import numpy as np
import ml_dtypes


def mxq(x, axis, fmt="e4m3"):
    dtype, down = {"e4m3": (ml_dtypes.float8_e4m3fn, 7), "e5m2": (ml_dtypes.float8_e5m2, 14)}[fmt]
    v = np.moveaxis(np.asarray(x, np.float32).astype(ml_dtypes.bfloat16).astype(np.float64), axis, -1)
    blocks = v.reshape(v.shape[:-1] + (-1, 32))
    amax = np.abs(blocks).max(-1, keepdims=True)
    byte = np.maximum(np.where(amax > 0, np.frexp(amax)[1] - 1 + 127, 0) - down, 1)
    scale = np.exp2(byte - 127.0)
    codes = (blocks / scale).astype(np.float32).astype(dtype).astype(np.float64)
    return np.moveaxis((codes * scale).reshape(v.shape), -1, axis)


WIDE = False


def mx_kscale(k, group=512):
    if not WIDE:
        return np.ones(k)
    levels = np.array([18, -18])
    if group != 512:
        return np.exp2(np.random.permutation(np.resize(levels, k // group))).repeat(group)
    if k % 512:
        return np.exp2(np.random.permutation(np.resize(levels, k // 32))).repeat(32)
    a = np.empty((k // 512, 16))
    for p in range(k // 512):
        a[p, :8] = np.random.permutation(np.resize(levels, 8))
        for g in range(8):
            far = levels[np.abs(levels - a[p, g]) >= 10]
            a[p, g + 8] = far[np.random.randint(len(far))]
    return np.exp2(a.ravel()).repeat(32)


def f64(x):
    return np.asarray(x).astype(np.float64)


def silu(v):
    return v / (1.0 + np.exp(-v))


G, D, K, M, N = 4, 128, 512, 128, 1024


def setup_inputs():
    n = np.random.standard_normal
    s = mx_kscale(D, 0)[:, None]
    u = mx_kscale(K)[:, None]
    return {
        "x": (n((G, D, N)) * s).astype(np.float32),
        "w1": (n((G, D, K)) / np.sqrt(D) / s).astype(np.float32),
        "hs": (np.random.uniform(0.5, 2.0, (G, K, 1)) * u).astype(np.float32),
        "w2": (n((G, K, M)) / np.sqrt(K) / u).astype(np.float32),
        "b": (0.5 * n((G, K, 1))).astype(np.float32),
    }


def reference(x, w1, hs, w2, b):
    xq = mxq(f64(x), 1, "e4m3")
    h = mxq(f64(w1), 1, "e4m3").transpose(0, 2, 1) @ xq
    h = h + f64(b)
    h = (silu(h)) * f64(hs)
    y = mxq(f64(w2), 1, "e4m3").transpose(0, 2, 1) @ mxq(h, 1, "e4m3")
    return y

@@ -1,0 +1,343 @@
+from contextlib import ExitStack
+
+import concourse.mybir as mybir
+
+G, D, K, M, N = 4, 128, 512, 128, 1024
+FLOPS = 2 * G * D * K * N + 2 * G * K * M * N
+
+F32 = mybir.dt.float32
+BF16 = mybir.dt.bfloat16
+U32 = mybir.dt.uint32
+U8 = mybir.dt.uint8
+FP8X4 = mybir.dt.float8_e4m3fn_x4
+ACT = mybir.ActivationFunctionType
+ALU = mybir.AluOpType
+
+P = 128
+PACK = 4
+ROWS = D // PACK
+NM = 128
+BANK = 512
+RUN = 4
+
+X_CHUNKS = [128, 128, 256, 256, 256]
+UNITS = [[0, 0, 512], [1, 0, 512], [2, 0, 512], [3, 0, 512], [0, 512, 512], [1, 512, 512], [2, 512, 512], [3, 512, 512]]
+BANKS_OF = [2, 2, 1, 1]
+PROGRAM = [
+    ["small"],
+    ["ldw1", 0],
+    ["ldw1", 1],
+    ["ldx", 0],
+    ["ldb"],
+    ["ldx", 1],
+    ["ldhs"],
+    ["ldx", 2],
+    ["ldx", 3],
+    ["ldx", 4],
+    ["ldw2", 0],
+    ["ldw2", 1],
+    ["cw1", 0, "v", 0, 64],
+    ["cw1", 1, "v", 0, 32],
+    ["cw1", 1, "a", 32, 64],
+    ["cx", 0, "v", 0, 128],
+    ["qw1", 0, 2],
+    ["qx", 0],
+    ["qw1", 2, 4],
+    ["cx", 1, "a", 0, 128],
+    ["mm1", 0, [0, 1], 0, 128],
+    ["mm1", 0, [2, 3], 0, 128],
+    ["mm1", 1, [0, 1, 2, 3], 0, 128],
+    ["silu", 0, [0], 0, 128],
+    ["silu", 0, [1], 0, 128],
+    ["silu", 0, [2], 0, 128],
+    ["mm1", 2, [0, 1, 2, 3], 0, 128],
+    ["cx", 2, "v", 0, 256],
+    ["silu", 0, [3], 0, 128],
+    ["silu", 1, [0], 0, 128],
+    ["mm1", 3, [0, 1, 2, 3], 0, 128],
+    ["silu", 1, [1], 0, 128],
+    ["qx", 1],
+    ["silu", 1, [2], 0, 128],
+    ["qx", 2],
+    ["silu", 1, [3], 0, 128],
+    ["silu", 2, [0], 0, 128],
+    ["tt", 0, 0, 128],
+    ["silu", 2, [1], 0, 128],
+    ["mm1", 1, [0], 128, 512],
+    ["silu", 2, [2], 0, 128],
+    ["cx", 3, "v", 0, 256],
+    ["silu", 2, [3], 0, 128],
+    ["silu", 3, [0], 0, 128],
+    ["mm1", 2, [0], 128, 512],
+    ["silu", 3, [1], 0, 128],
+    ["tt", 1, 0, 128],
+    ["silu", 3, [2], 0, 128],
+    ["mm1", 1, [1], 128, 512],
+    ["silu", 3, [3], 0, 128],
+    ["silu", 1, [0], 128, 512],
+    ["qx", 3],
+    ["tt", 2, 0, 128],
+    ["silu", 2, [0], 128, 512],
+    ["mm1", 1, [2], 128, 512],
+    ["silu", 1, [1], 128, 512],
+    ["cx", 4, "v", 0, 256],
+    ["mm1", 2, [1], 128, 512],
+    ["silu", 1, [2], 128, 512],
+    ["mm1", 1, [3], 128, 512],
+    ["tt", 3, 0, 128],
+    ["silu", 2, [1], 128, 512],
+    ["mm1", 3, [0], 128, 512],
+    ["qx", 4],
+    ["silu", 1, [3], 128, 512],
+    ["cw2", 1, "v"],
+    ["mm1", 2, [2], 128, 512],
+    ["silu", 3, [0], 128, 512],
+    ["mm1", 0, [0], 128, 512],
+    ["tt", 1, 128, 512],
+    ["silu", 2, [2], 128, 512],
+    ["mm1", 3, [1], 128, 512],
+    ["silu", 0, [0], 128, 512],
+    ["mm1", 2, [3], 128, 512],
+    ["silu", 3, [1], 128, 512],
+    ["cw2", 2, "v"],
+    ["silu", 2, [3], 128, 512],
+    ["mm1", 3, [2], 128, 512],
+    ["cw2", 3, "v"],
+    ["cw2", 0, "a"],
+    ["mm1", 6, [0], 0, 512],
+    ["tt", 2, 128, 512],
+    ["mm1", 0, [1], 128, 512],
+    ["silu", 3, [2], 128, 512],
+    ["silu", 6, [0], 0, 512],
+    ["mm1", 3, [3], 128, 512],
+    ["silu", 0, [1], 128, 512],
+    ["mm1", 6, [1], 0, 512],
+    ["qw2", 0],
+    ["qh", 1, 0, 512],
+    ["silu", 3, [3], 128, 512],
+    ["mm1", 0, [2], 128, 512],
+    ["silu", 6, [1], 0, 512],
+    ["mm1", 0, [3], 128, 512],
+    ["tt", 3, 128, 512],
+    ["silu", 0, [2], 128, 512],
+    ["mm1", 6, [2], 0, 512],
+    ["silu", 0, [3], 128, 512],
+    ["mm1", 5, [0], 0, 512],
+    ["silu", 6, [2], 0, 512],
+    ["mm1", 5, [1], 0, 512],
+    ["qw2", 1],
+    ["silu", 5, [0], 0, 512],
+    ["qh", 2, 0, 512],
+    ["mm1", 6, [3], 0, 512],
+    ["tt", 0, 128, 512],
+    ["silu", 5, [1], 0, 512],
+    ["mm1", 5, [2], 0, 512],
+    ["silu", 6, [3], 0, 512],
+    ["mm1", 5, [3], 0, 512],
+    ["silu", 5, [2], 0, 512],
+    ["mm2", 1, 0, 512, 0],
+    ["qh", 3, 0, 512],
+    ["silu", 5, [3], 0, 512],
+    ["mm1", 4, [0], 0, 512],
+    ["tt", 6, 0, 512],
+    ["ev", 1, 0, 512, 0, "a"],
+    ["mm1", 4, [1], 0, 512],
+    ["mm1", 7, [0], 0, 512],
+    ["silu", 4, [0], 0, 512],
+    ["st", 1, 0, 512],
+    ["silu", 4, [1], 0, 512],
+    ["mm1", 4, [2], 0, 512],
+    ["silu", 7, [0], 0, 512],
+    ["mm1", 4, [3], 0, 512],
+    ["qh", 0, 0, 512],
+    ["silu", 4, [2], 0, 512],
+    ["mm1", 7, [1], 0, 512],
+    ["tt", 5, 0, 512],
+    ["silu", 4, [3], 0, 512],
+    ["mm2", 2, 0, 512, 1],
+    ["silu", 7, [1], 0, 512],
+    ["ev", 2, 0, 512, 1, "a"],
+    ["mm1", 7, [2], 0, 512],
+    ["qh", 6, 0, 512],
+    ["st", 2, 0, 512],
+    ["silu", 7, [2], 0, 512],
+    ["tt", 4, 0, 512],
+    ["mm1", 7, [3], 0, 512],
+    ["mm2", 3, 0, 512, 0],
+    ["silu", 7, [3], 0, 512],
+    ["mm2", 0, 0, 512, 1],
+    ["ev", 3, 0, 512, 0, "a"],
+    ["qh", 5, 0, 512],
+    ["ev", 0, 0, 512, 1, "a"],
+    ["mm2", 6, 0, 512, 0],
+    ["tt", 7, 0, 256],
+    ["st", 3, 0, 512],
+    ["mm2", 5, 0, 512, 1],
+    ["st", 0, 0, 512],
+    ["ev", 6, 0, 512, 0, "a"],
+    ["qh", 4, 0, 512],
+    ["ev", 5, 0, 512, 1, "a"],
+    ["st", 6, 0, 512],
+    ["tt", 7, 256, 384],
+    ["mm2", 4, 0, 512, 0],
+    ["st", 5, 0, 512],
+    ["qh", 7, 0, 256],
+    ["tt", 7, 384, 512],
+    ["ev", 4, 0, 512, 0, "a"],
+    ["mm2", 7, 0, 256, 1],
+    ["qh", 7, 256, 384],
+    ["qh", 7, 384, 512],
+    ["ev", 7, 0, 256, 1, "a"],
+    ["mm2", 7, 256, 384, 0],
+    ["st", 4, 0, 512],
+    ["mm2", 7, 384, 512, 1],
+    ["st", 7, 0, 256],
+    ["ev", 7, 256, 384, 0, "v"],
+    ["ev", 7, 384, 512, 1, "v"],
+    ["st", 7, 256, 384],
+    ["st", 7, 384, 512],
+]
+
+
+def tile_rows_gmlp_silu_bias_kernel(tc, x, w1, hs, w2, b, out):
+    nc = tc.nc
+    with ExitStack() as ctx:
+        keep = ctx.enter_context(tc.tile_pool(name="keep", bufs=1))
+        psum = ctx.enter_context(tc.psum_pool(name="psum", bufs=1))
+        ctx.enter_context(tc.manual_schedule())
+
+        def sb(name, shape, dtype):
+            return keep.tile(shape, dtype, name=name, align_bytes=64)
+
+        x_rows = x.rearrange("g (p j) n -> (g p) j n", j=PACK)
+        w1_rows = w1.rearrange("g (p j) k -> (g p) j k", j=PACK)
+        w2_rows = w2.rearrange("g (p j) m -> p g j m", j=PACK)
+
+        x_start = [sum(X_CHUNKS[:i]) for i in range(len(X_CHUNKS))]
+        x_raw = [sb("x_raw%d" % i, [P, PACK, w], F32) for i, w in enumerate(X_CHUNKS)]
+        x_bf = [sb("x_bf%d" % i, [P, w * PACK], BF16) for i, w in enumerate(X_CHUNKS)]
+        x_codes = [sb("x_codes%d" % i, [P, w], U32) for i, w in enumerate(X_CHUNKS)]
+        x_scales = [sb("x_scales%d" % i, [P, w], U8) for i, w in enumerate(X_CHUNKS)]
+        w1_raw = [sb("w1_raw%d" % i, [P, PACK, K // 2], F32) for i in range(2)]
+        w1_bf = sb("w1_bf", [P, K * PACK], BF16)
+        w1_codes = sb("w1_codes", [P, K], U32)
+        w1_scales = sb("w1_scales", [P, K], U8)
+        w2_raw = [sb("w2_raw%d" % i, [P, 2, PACK, M], F32) for i in range(2)]
+        w2_bf = [sb("w2_bf%d" % i, [P, 2 * M * PACK], BF16) for i in range(2)]
+        w2_codes = [sb("w2_codes%d" % i, [P, 2 * M], U32) for i in range(2)]
+        w2_scales = [sb("w2_scales%d" % i, [P, 2 * M], U8) for i in range(2)]
+        b_sb = sb("b_sb", [P, G, 8], F32)
+        hs_sb = sb("hs_sb", [P, G, 8], F32)
+        warm = sb("warm", [P, 8], F32)
+        act = [sb("act%d" % u, [P, PACK, w], F32) for u, (g, n0, w) in enumerate(UNITS)]
+        h_bf = [sb("h_bf%d" % u, [P, w * PACK], BF16) for u, (g, n0, w) in enumerate(UNITS)]
+        h_codes = [sb("h_codes%d" % u, [P, w], U32) for u, (g, n0, w) in enumerate(UNITS)]
+        h_scales = [sb("h_scales%d" % u, [P, w], U8) for u, (g, n0, w) in enumerate(UNITS)]
+        res = [sb("res%d" % u, [P, w], F32) for u, (g, n0, w) in enumerate(UNITS)]
+        z_banks = [[psum.tile([P, BANK], F32, name="bank_z%d_%d" % (g, i)) for i in range(BANKS_OF[g])] for g in range(G)]
+        y_banks = [psum.tile([P, BANK], F32, name="bank_y%d" % i) for i in range(8 - sum(BANKS_OF))]
+        fills = [0] * G
+        where = {}
+
+        def copy(eng, out, in_):
+            if eng == "v":
+                nc.vector.tensor_copy(out=out, in_=in_)
+            else:
+                nc.scalar.copy(out=out, in_=in_)
+
+        def quant(codes, scales, src):
+            nc.vector.quantize_mx(out=codes.bitcast(FP8X4), scales=scales, in_=src)
+
+        for step in PROGRAM:
+            kind = step[0]
+            if kind == "ldx":
+                i = step[1]
+                nc.sync.dma_start(out=x_raw[i][:], in_=x_rows[:, :, x_start[i] : x_start[i] + X_CHUNKS[i]])
+            elif kind == "ldw1":
+                i = step[1]
+                nc.sync.dma_start(out=w1_raw[i][:], in_=w1_rows[:, :, i * 256 : i * 256 + 256])
+            elif kind == "ldw2":
+                i = step[1]
+                nc.sync.dma_start(out=w2_raw[i][:].rearrange("p g j m -> p g (j m)"), in_=w2_rows[:, 2 * i : 2 * i + 2].rearrange("p g j m -> p g (j m)"))
+            elif kind == "small":
+                nc.vector.memset(warm[:, 0:1], 0.0)
+                nc.scalar.activation(out=warm[:, 4:5], in_=warm[:, 0:1], func=ACT.Silu)
+            elif kind == "ldb":
+                nc.sync.dma_start(out=b_sb[:, :, 0:PACK], in_=b.rearrange("g (p r) o -> p g (r o)", r=PACK))
+            elif kind == "ldhs":
+                nc.sync.dma_start(out=hs_sb[:, :, 0:PACK], in_=hs.rearrange("g (p r) o -> p g (r o)", r=PACK))
+            elif kind == "cx":
+                i, eng, c0, c1 = step[1:]
+                copy(eng, x_bf[i][:, PACK * c0 : PACK * c1].rearrange("p (c i j) -> p c j i", i=RUN, j=PACK), x_raw[i][:, :, c0:c1].rearrange("p j (c i) -> p c j i", i=RUN))
+            elif kind == "qx":
+                i = step[1]
+                quant(x_codes[i][:], x_scales[i][:], x_bf[i][:])
+            elif kind == "cw1":
+                i, eng, s0, s1 = step[1:]
+                dst = w1_bf[:].rearrange("p (r s j) -> p s j r", r=PACK, j=PACK)[:, 64 * i + s0 : 64 * i + s1]
+                copy(eng, dst, w1_raw[i][:].rearrange("p j (s r) -> p s j r", r=PACK)[:, s0:s1])
+            elif kind == "qw1":
+                r0, r1 = step[1:]
+                quant(w1_codes[:, r0 * P : r1 * P], w1_scales[:, r0 * P : r1 * P], w1_bf[:, r0 * P * PACK : r1 * P * PACK])
+            elif kind == "cw2":
+                i, gg, eng = step[1] // 2, step[1] % 2, step[2]
+                dst = w2_bf[i][:, gg * 512 : gg * 512 + 512].rearrange("p (c i j) -> p c j i", i=RUN, j=PACK)
+                copy(eng, dst, w2_raw[i][:, gg].rearrange("p j (c i) -> p c j i", i=RUN))
+            elif kind == "qw2":
+                i = step[1]
+                quant(w2_codes[i][:], w2_scales[i][:], w2_bf[i][:])
+            elif kind == "mm1":
+                u, rs, c0, c1 = step[1:]
+                g, n0, w = UNITS[u]
+                n0, w = n0 + c0, c1 - c0
+                bank = z_banks[g][fills[g] % BANKS_OF[g]]
+                fills[g] += 1
+                rows = slice(ROWS * g, ROWS * g + ROWS)
+                for a, r in enumerate(rs):
+                    where[(u, r, c0)] = bank[:, a * w : a * w + w]
+                    for c in range(0, w, NM):
+                        i = max(t for t in range(len(X_CHUNKS)) if x_start[t] <= n0 + c)
+                        o = n0 + c - x_start[i]
+                        nc.tensor.matmul_mx(
+                            out=bank[:, a * w + c : a * w + c + NM],
+                            lhsT=w1_codes[rows, r * P : r * P + P].bitcast(FP8X4),
+                            lhsT_scale=w1_scales[rows, r * P : r * P + P],
+                            rhs=x_codes[i][rows, o : o + NM].bitcast(FP8X4),
+                            rhs_scale=x_scales[i][rows, o : o + NM],
+                            start=True, stop=True)
+            elif kind == "silu":
+                u, rs, c0, c1 = step[1:]
+                g, n0, w = UNITS[u]
+                for r in rs:
+                    nc.scalar.activation(out=act[u][:, r, c0:c1], in_=where[(u, r, c0)], func=ACT.Silu, bias=b_sb[:, g, r : r + 1])
+            elif kind == "tt":
+                u, c0, c1 = step[1:]
+                g, n0, w = UNITS[u]
+                nc.vector.tensor_tensor(
+                    out=h_bf[u][:, PACK * c0 : PACK * c1].rearrange("p (c i r) -> p c r i", i=RUN, r=PACK),
+                    in0=act[u][:, :, c0:c1].rearrange("p r (c i) -> p c r i", i=RUN),
+                    in1=hs_sb[:, g, 0:PACK].unsqueeze(1).unsqueeze(3).to_broadcast([P, (c1 - c0) // RUN, PACK, RUN]),
+                    op=ALU.mult)
+            elif kind == "qh":
+                u, c0, c1 = step[1:]
+                quant(h_codes[u][:, c0:c1], h_scales[u][:, c0:c1], h_bf[u][:, PACK * c0 : PACK * c1])
+            elif kind == "mm2":
+                u, c0, c1, bk = step[1:]
+                g, n0, w = UNITS[u]
+                wc = slice((g % 2) * M, (g % 2) * M + M)
+                for c in range(c0, c1, NM):
+                    nc.tensor.matmul_mx(
+                        out=y_banks[bk][:, c : c + NM],
+                        lhsT=w2_codes[g // 2][:, wc].bitcast(FP8X4),
+                        lhsT_scale=w2_scales[g // 2][:, wc],
+                        rhs=h_codes[u][:, c : c + NM].bitcast(FP8X4),
+                        rhs_scale=h_scales[u][:, c : c + NM],
+                        start=True, stop=True)
+            elif kind == "ev":
+                u, c0, c1, bk, eng = step[1:]
+                g, n0, w = UNITS[u]
+                copy(eng, res[u][:, c0:c1], y_banks[bk][:, c0:c1])
+            elif kind == "st":
+                u, c0, c1 = step[1:]
+                g, n0, w = UNITS[u]
+                nc.sync.dma_start(out=out[g, :, n0 + c0 : n0 + c1], in_=res[u][:, c0:c1])

@@ -16,186 +16,147 @@ ALU = mybir.AluOpType
 P = 128
 PACK = 4
 ROWS = D // PACK
-NM = 128
+NM = 512
 BANK = 512
 RUN = 4
 
-X_CHUNKS = [128, 128, 256, 256, 256]
+X_CHUNKS = [256, 256, 512]
 UNITS = [[0, 0, 512], [1, 0, 512], [2, 0, 512], [3, 0, 512], [0, 512, 512], [1, 512, 512], [2, 512, 512], [3, 512, 512]]
 BANKS_OF = [2, 2, 1, 1]
 PROGRAM = [
     ["small"],
-    ["ldw1", 0],
-    ["ldw1", 1],
+    ["ldw1", 0, 128],
     ["ldx", 0],
-    ["ldb"],
     ["ldx", 1],
-    ["ldhs"],
+    ["ldb", "s"],
     ["ldx", 2],
-    ["ldx", 3],
-    ["ldx", 4],
+    ["ldhs", "s"],
     ["ldw2", 0],
     ["ldw2", 1],
-    ["cw1", 0, "v", 0, 64],
-    ["cw1", 1, "v", 0, 32],
-    ["cw1", 1, "a", 32, 64],
-    ["cx", 0, "v", 0, 128],
-    ["qw1", 0, 2],
-    ["qx", 0],
-    ["qw1", 2, 4],
-    ["cx", 1, "a", 0, 128],
-    ["mm1", 0, [0, 1], 0, 128],
-    ["mm1", 0, [2, 3], 0, 128],
-    ["mm1", 1, [0, 1, 2, 3], 0, 128],
-    ["silu", 0, [0], 0, 128],
-    ["silu", 0, [1], 0, 128],
-    ["silu", 0, [2], 0, 128],
-    ["mm1", 2, [0, 1, 2, 3], 0, 128],
-    ["cx", 2, "v", 0, 256],
-    ["silu", 0, [3], 0, 128],
-    ["silu", 1, [0], 0, 128],
-    ["mm1", 3, [0, 1, 2, 3], 0, 128],
-    ["silu", 1, [1], 0, 128],
-    ["qx", 1],
-    ["silu", 1, [2], 0, 128],
-    ["qx", 2],
-    ["silu", 1, [3], 0, 128],
-    ["silu", 2, [0], 0, 128],
-    ["tt", 0, 0, 128],
-    ["silu", 2, [1], 0, 128],
-    ["mm1", 1, [0], 128, 512],
-    ["silu", 2, [2], 0, 128],
-    ["cx", 3, "v", 0, 256],
-    ["silu", 2, [3], 0, 128],
-    ["silu", 3, [0], 0, 128],
-    ["mm1", 2, [0], 128, 512],
-    ["silu", 3, [1], 0, 128],
-    ["tt", 1, 0, 128],
-    ["silu", 3, [2], 0, 128],
-    ["mm1", 1, [1], 128, 512],
-    ["silu", 3, [3], 0, 128],
-    ["silu", 1, [0], 128, 512],
-    ["qx", 3],
-    ["tt", 2, 0, 128],
-    ["silu", 2, [0], 128, 512],
-    ["mm1", 1, [2], 128, 512],
-    ["silu", 1, [1], 128, 512],
-    ["cx", 4, "v", 0, 256],
-    ["mm1", 2, [1], 128, 512],
-    ["silu", 1, [2], 128, 512],
-    ["mm1", 1, [3], 128, 512],
-    ["tt", 3, 0, 128],
-    ["silu", 2, [1], 128, 512],
-    ["mm1", 3, [0], 128, 512],
-    ["qx", 4],
-    ["silu", 1, [3], 128, 512],
-    ["cw2", 1, "v"],
-    ["mm1", 2, [2], 128, 512],
-    ["silu", 3, [0], 128, 512],
-    ["mm1", 0, [0], 128, 512],
-    ["tt", 1, 128, 512],
-    ["silu", 2, [2], 128, 512],
-    ["mm1", 3, [1], 128, 512],
-    ["silu", 0, [0], 128, 512],
-    ["mm1", 2, [3], 128, 512],
-    ["silu", 3, [1], 128, 512],
-    ["cw2", 2, "v"],
-    ["silu", 2, [3], 128, 512],
-    ["mm1", 3, [2], 128, 512],
-    ["cw2", 3, "v"],
-    ["cw2", 0, "a"],
-    ["mm1", 6, [0], 0, 512],
-    ["tt", 2, 128, 512],
-    ["mm1", 0, [1], 128, 512],
-    ["silu", 3, [2], 128, 512],
-    ["silu", 6, [0], 0, 512],
-    ["mm1", 3, [3], 128, 512],
-    ["silu", 0, [1], 128, 512],
-    ["mm1", 6, [1], 0, 512],
-    ["qw2", 0],
-    ["qh", 1, 0, 512],
-    ["silu", 3, [3], 128, 512],
-    ["mm1", 0, [2], 128, 512],
-    ["silu", 6, [1], 0, 512],
-    ["mm1", 0, [3], 128, 512],
-    ["tt", 3, 128, 512],
-    ["silu", 0, [2], 128, 512],
-    ["mm1", 6, [2], 0, 512],
-    ["silu", 0, [3], 128, 512],
-    ["mm1", 5, [0], 0, 512],
-    ["silu", 6, [2], 0, 512],
-    ["mm1", 5, [1], 0, 512],
-    ["qw2", 1],
-    ["silu", 5, [0], 0, 512],
-    ["qh", 2, 0, 512],
-    ["mm1", 6, [3], 0, 512],
-    ["tt", 0, 128, 512],
-    ["silu", 5, [1], 0, 512],
-    ["mm1", 5, [2], 0, 512],
-    ["silu", 6, [3], 0, 512],
-    ["mm1", 5, [3], 0, 512],
-    ["silu", 5, [2], 0, 512],
-    ["mm2", 1, 0, 512, 0],
-    ["qh", 3, 0, 512],
-    ["silu", 5, [3], 0, 512],
+    ["cw1", 0, "v", 0, 96],
+    ["cw1", 0, "a", 96, 128],
+    ["cx", 0, "v", 0, 256],
+    ["qw1", 0, 4],
+    ["cx", 1, "a", 160, 256],
+    ["cx", 1, "v", 0, 160],
+    ["qx", 0, 0, 256],
+    ["qx", 1, 0, 256],
+    ["mm1", 0, [0], 0, 512],
+    ["mm1", 0, [1], 0, 512],
+    ["mm1", 1, [0], 0, 512],
+    ["silu", 0, [0], 0, 512],
+    ["cx", 2, "v", 0, 512],
+    ["silu", 0, [1], 0, 512],
+    ["mm1", 0, [2], 0, 512],
+    ["silu", 1, [0], 0, 512],
+    ["mm1", 0, [3], 0, 512],
+    ["mm1", 1, [1], 0, 512],
+    ["silu", 0, [2], 0, 512],
+    ["qx", 2, 0, 512],
+    ["mm1", 1, [2], 0, 512],
+    ["mm1", 2, [0], 0, 512],
+    ["silu", 0, [3], 0, 512],
+    ["silu", 1, [1], 0, 512],
+    ["tt", 0, 0, 512],
+    ["silu", 1, [2], 0, 512],
+    ["mm1", 1, [3], 0, 512],
     ["mm1", 4, [0], 0, 512],
-    ["tt", 6, 0, 512],
-    ["ev", 1, 0, 512, 0, "a"],
+    ["silu", 2, [0], 0, 512],
+    ["silu", 1, [3], 0, 512],
+    ["mm1", 2, [1], 0, 512],
     ["mm1", 4, [1], 0, 512],
-    ["mm1", 7, [0], 0, 512],
     ["silu", 4, [0], 0, 512],
-    ["st", 1, 0, 512],
-    ["silu", 4, [1], 0, 512],
+    ["cw2", 0, "v"],
+    ["cw2", 1, "v"],
+    ["silu", 2, [1], 0, 512],
+    ["tt", 1, 0, 512],
     ["mm1", 4, [2], 0, 512],
-    ["silu", 7, [0], 0, 512],
-    ["mm1", 4, [3], 0, 512],
-    ["qh", 0, 0, 512],
+    ["silu", 4, [1], 0, 512],
+    ["mm1", 2, [2], 0, 512],
     ["silu", 4, [2], 0, 512],
-    ["mm1", 7, [1], 0, 512],
-    ["tt", 5, 0, 512],
+    ["mm1", 4, [3], 0, 512],
+    ["mm1", 3, [0], 0, 512],
+    ["silu", 2, [2], 0, 512],
+    ["qw2", 0],
     ["silu", 4, [3], 0, 512],
-    ["mm2", 2, 0, 512, 1],
-    ["silu", 7, [1], 0, 512],
-    ["ev", 2, 0, 512, 1, "a"],
-    ["mm1", 7, [2], 0, 512],
-    ["qh", 6, 0, 512],
-    ["st", 2, 0, 512],
-    ["silu", 7, [2], 0, 512],
+    ["qh", 0, 0, 512],
+    ["mm1", 2, [3], 0, 512],
+    ["mm1", 5, [0], 0, 512],
+    ["silu", 3, [0], 0, 512],
     ["tt", 4, 0, 512],
-    ["mm1", 7, [3], 0, 512],
-    ["mm2", 3, 0, 512, 0],
-    ["silu", 7, [3], 0, 512],
-    ["mm2", 0, 0, 512, 1],
-    ["ev", 3, 0, 512, 0, "a"],
-    ["qh", 5, 0, 512],
-    ["ev", 0, 0, 512, 1, "a"],
-    ["mm2", 6, 0, 512, 0],
-    ["tt", 7, 0, 256],
-    ["st", 3, 0, 512],
-    ["mm2", 5, 0, 512, 1],
-    ["st", 0, 0, 512],
-    ["ev", 6, 0, 512, 0, "a"],
+    ["silu", 2, [3], 0, 512],
+    ["mm1", 3, [1], 0, 512],
+    ["mm1", 5, [1], 0, 512],
+    ["silu", 5, [0], 0, 512],
+    ["silu", 3, [1], 0, 512],
+    ["mm1", 5, [2], 0, 512],
+    ["silu", 5, [1], 0, 512],
+    ["qh", 1, 0, 512],
+    ["mm1", 3, [2], 0, 512],
+    ["tt", 2, 0, 512],
+    ["silu", 5, [2], 0, 512],
+    ["mm1", 5, [3], 0, 512],
+    ["mm1", 6, [0], 0, 512],
+    ["silu", 3, [2], 0, 512],
+    ["silu", 5, [3], 0, 512],
+    ["mm1", 3, [3], 0, 512],
+    ["silu", 6, [0], 0, 512],
     ["qh", 4, 0, 512],
-    ["ev", 5, 0, 512, 1, "a"],
-    ["st", 6, 0, 512],
-    ["tt", 7, 256, 384],
+    ["cw2", 2, "a"],
+    ["mm1", 6, [1], 0, 512],
+    ["tt", 5, 0, 512],
+    ["silu", 3, [3], 0, 512],
+    ["silu", 6, [1], 0, 512],
+    ["mm1", 7, [0], 0, 512],
+    ["cw2", 3, "a"],
+    ["mm1", 6, [2], 0, 512],
+    ["silu", 7, [0], 0, 512],
+    ["qh", 2, 0, 512],
+    ["mm2", 0, 0, 512, 0],
+    ["silu", 6, [2], 0, 512],
+    ["tt", 3, 0, 512],
+    ["mm1", 7, [1], 0, 512],
+    ["ev", 0, 0, 512, 0, "a"],
+    ["mm1", 6, [3], 0, 512],
+    ["silu", 7, [1], 0, 512],
+    ["mm2", 1, 0, 512, 1],
+    ["st", 0, 0, 512],
+    ["silu", 6, [3], 0, 512],
+    ["mm1", 7, [2], 0, 512],
+    ["qh", 5, 0, 512],
+    ["ev", 1, 0, 512, 1, "a"],
+    ["tt", 6, 0, 512],
+    ["silu", 7, [2], 0, 512],
+    ["st", 1, 0, 512],
+    ["mm1", 7, [3], 0, 512],
     ["mm2", 4, 0, 512, 0],
-    ["st", 5, 0, 512],
-    ["qh", 7, 0, 256],
-    ["tt", 7, 384, 512],
+    ["silu", 7, [3], 0, 512],
+    ["qw2", 1],
     ["ev", 4, 0, 512, 0, "a"],
-    ["mm2", 7, 0, 256, 1],
-    ["qh", 7, 256, 384],
-    ["qh", 7, 384, 512],
-    ["ev", 7, 0, 256, 1, "a"],
-    ["mm2", 7, 256, 384, 0],
+    ["qh", 3, 0, 512],
+    ["mm2", 2, 0, 512, 1],
+    ["tt", 7, 0, 256],
     ["st", 4, 0, 512],
-    ["mm2", 7, 384, 512, 1],
+    ["mm2", 5, 0, 512, 0],
+    ["ev", 2, 0, 512, 1, "a"],
+    ["qh", 6, 0, 512],
+    ["ev", 5, 0, 512, 0, "a"],
+    ["mm2", 3, 0, 512, 1],
+    ["st", 2, 0, 512],
+    ["tt", 7, 256, 512],
+    ["mm2", 6, 0, 512, 0],
+    ["st", 5, 0, 512],
+    ["ev", 3, 0, 512, 1, "a"],
+    ["qh", 7, 0, 256],
+    ["ev", 6, 0, 512, 0, "a"],
+    ["st", 3, 0, 512],
+    ["qh", 7, 256, 512],
+    ["st", 6, 0, 512],
+    ["mm2", 7, 0, 512, 1],
+    ["ev", 7, 0, 256, 1, "a"],
+    ["ev", 7, 256, 512, 1, "a"],
     ["st", 7, 0, 256],
-    ["ev", 7, 256, 384, 0, "v"],
-    ["ev", 7, 384, 512, 1, "v"],
-    ["st", 7, 256, 384],
-    ["st", 7, 384, 512],
+    ["st", 7, 256, 512],
 ]
 
 
@@ -216,9 +177,9 @@ def tile_rows_gmlp_silu_bias_kernel(tc, x, w1, hs, w2, b, out):
         x_start = [sum(X_CHUNKS[:i]) for i in range(len(X_CHUNKS))]
         x_raw = [sb("x_raw%d" % i, [P, PACK, w], F32) for i, w in enumerate(X_CHUNKS)]
         x_bf = [sb("x_bf%d" % i, [P, w * PACK], BF16) for i, w in enumerate(X_CHUNKS)]
-        x_codes = [sb("x_codes%d" % i, [P, w], U32) for i, w in enumerate(X_CHUNKS)]
-        x_scales = [sb("x_scales%d" % i, [P, w], U8) for i, w in enumerate(X_CHUNKS)]
-        w1_raw = [sb("w1_raw%d" % i, [P, PACK, K // 2], F32) for i in range(2)]
+        x_codes = sb("x_codes", [P, N], U32)
+        x_scales = sb("x_scales", [P, N], U8)
+        w1_raw = sb("w1_raw", [P, PACK, K], F32)
         w1_bf = sb("w1_bf", [P, K * PACK], BF16)
         w1_codes = sb("w1_codes", [P, K], U32)
         w1_scales = sb("w1_scales", [P, K], U8)
@@ -229,7 +190,10 @@ def tile_rows_gmlp_silu_bias_kernel(tc, x, w1, hs, w2, b, out):
         b_sb = sb("b_sb", [P, G, 8], F32)
         hs_sb = sb("hs_sb", [P, G, 8], F32)
         warm = sb("warm", [P, 8], F32)
-        act = [sb("act%d" % u, [P, PACK, w], F32) for u, (g, n0, w) in enumerate(UNITS)]
+        act = {}
+        for step in PROGRAM:
+            if step[0] == "silu" and (step[1], step[3]) not in act:
+                act[(step[1], step[3])] = sb("act%d_%d" % (step[1], step[3]), [P, PACK, step[4] - step[3]], F32)
         h_bf = [sb("h_bf%d" % u, [P, w * PACK], BF16) for u, (g, n0, w) in enumerate(UNITS)]
         h_codes = [sb("h_codes%d" % u, [P, w], U32) for u, (g, n0, w) in enumerate(UNITS)]
         h_scales = [sb("h_scales%d" % u, [P, w], U8) for u, (g, n0, w) in enumerate(UNITS)]
@@ -254,8 +218,8 @@ def tile_rows_gmlp_silu_bias_kernel(tc, x, w1, hs, w2, b, out):
                 i = step[1]
                 nc.sync.dma_start(out=x_raw[i][:], in_=x_rows[:, :, x_start[i] : x_start[i] + X_CHUNKS[i]])
             elif kind == "ldw1":
-                i = step[1]
-                nc.sync.dma_start(out=w1_raw[i][:], in_=w1_rows[:, :, i * 256 : i * 256 + 256])
+                s0, s1 = step[1:]
+                nc.sync.dma_start(out=w1_raw[:, :, 4 * s0 : 4 * s1], in_=w1_rows[:, :, 4 * s0 : 4 * s1])
             elif kind == "ldw2":
                 i = step[1]
                 nc.sync.dma_start(out=w2_raw[i][:].rearrange("p g j m -> p g (j m)"), in_=w2_rows[:, 2 * i : 2 * i + 2].rearrange("p g j m -> p g (j m)"))
@@ -263,19 +227,19 @@ def tile_rows_gmlp_silu_bias_kernel(tc, x, w1, hs, w2, b, out):
                 nc.vector.memset(warm[:, 0:1], 0.0)
                 nc.scalar.activation(out=warm[:, 4:5], in_=warm[:, 0:1], func=ACT.Silu)
             elif kind == "ldb":
-                nc.sync.dma_start(out=b_sb[:, :, 0:PACK], in_=b.rearrange("g (p r) o -> p g (r o)", r=PACK))
+                (nc.sync if step[1] == "s" else nc.scalar).dma_start(out=b_sb[:, :, 0:PACK], in_=b.rearrange("g (p r) o -> p g (r o)", r=PACK))
             elif kind == "ldhs":
-                nc.sync.dma_start(out=hs_sb[:, :, 0:PACK], in_=hs.rearrange("g (p r) o -> p g (r o)", r=PACK))
+                (nc.sync if step[1] == "s" else nc.scalar).dma_start(out=hs_sb[:, :, 0:PACK], in_=hs.rearrange("g (p r) o -> p g (r o)", r=PACK))
             elif kind == "cx":
                 i, eng, c0, c1 = step[1:]
                 copy(eng, x_bf[i][:, PACK * c0 : PACK * c1].rearrange("p (c i j) -> p c j i", i=RUN, j=PACK), x_raw[i][:, :, c0:c1].rearrange("p j (c i) -> p c j i", i=RUN))
             elif kind == "qx":
-                i = step[1]
-                quant(x_codes[i][:], x_scales[i][:], x_bf[i][:])
+                i, c0, c1 = step[1:]
+                quant(x_codes[:, x_start[i] + c0 : x_start[i] + c1], x_scales[:, x_start[i] + c0 : x_start[i] + c1], x_bf[i][:, PACK * c0 : PACK * c1])
             elif kind == "cw1":
                 i, eng, s0, s1 = step[1:]
-                dst = w1_bf[:].rearrange("p (r s j) -> p s j r", r=PACK, j=PACK)[:, 64 * i + s0 : 64 * i + s1]
-                copy(eng, dst, w1_raw[i][:].rearrange("p j (s r) -> p s j r", r=PACK)[:, s0:s1])
+                dst = w1_bf[:].rearrange("p (r s j) -> p s j r", r=PACK, j=PACK)[:, s0:s1]
+                copy(eng, dst, w1_raw[:].rearrange("p j (s r) -> p s j r", r=PACK)[:, s0:s1])
             elif kind == "qw1":
                 r0, r1 = step[1:]
                 quant(w1_codes[:, r0 * P : r1 * P], w1_scales[:, r0 * P : r1 * P], w1_bf[:, r0 * P * PACK : r1 * P * PACK])
@@ -296,26 +260,26 @@ def tile_rows_gmlp_silu_bias_kernel(tc, x, w1, hs, w2, b, out):
                 for a, r in enumerate(rs):
                     where[(u, r, c0)] = bank[:, a * w : a * w + w]
                     for c in range(0, w, NM):
-                        i = max(t for t in range(len(X_CHUNKS)) if x_start[t] <= n0 + c)
-                        o = n0 + c - x_start[i]
+                        o = n0 + c
                         nc.tensor.matmul_mx(
                             out=bank[:, a * w + c : a * w + c + NM],
                             lhsT=w1_codes[rows, r * P : r * P + P].bitcast(FP8X4),
                             lhsT_scale=w1_scales[rows, r * P : r * P + P],
-                            rhs=x_codes[i][rows, o : o + NM].bitcast(FP8X4),
-                            rhs_scale=x_scales[i][rows, o : o + NM],
+                            rhs=x_codes[rows, o : o + NM].bitcast(FP8X4),
+                            rhs_scale=x_scales[rows, o : o + NM],
                             start=True, stop=True)
             elif kind == "silu":
                 u, rs, c0, c1 = step[1:]
                 g, n0, w = UNITS[u]
                 for r in rs:
-                    nc.scalar.activation(out=act[u][:, r, c0:c1], in_=where[(u, r, c0)], func=ACT.Silu, bias=b_sb[:, g, r : r + 1])
+                    nc.scalar.activation(out=act[(u, c0)][:, r, :], in_=where[(u, r, c0)], func=ACT.Silu, bias=b_sb[:, g, r : r + 1])
             elif kind == "tt":
                 u, c0, c1 = step[1:]
                 g, n0, w = UNITS[u]
+                a0 = max(c for (v, c) in act if v == u and c <= c0)
                 nc.vector.tensor_tensor(
                     out=h_bf[u][:, PACK * c0 : PACK * c1].rearrange("p (c i r) -> p c r i", i=RUN, r=PACK),
-                    in0=act[u][:, :, c0:c1].rearrange("p r (c i) -> p c r i", i=RUN),
+                    in0=act[(u, a0)][:, :, c0 - a0 : c1 - a0].rearrange("p r (c i) -> p c r i", i=RUN),
                     in1=hs_sb[:, g, 0:PACK].unsqueeze(1).unsqueeze(3).to_broadcast([P, (c1 - c0) // RUN, PACK, RUN]),
                     op=ALU.mult)
             elif kind == "qh":

@@ -10,154 +10,22 @@ BF16 = mybir.dt.bfloat16
 U32 = mybir.dt.uint32
 U8 = mybir.dt.uint8
 FP8X4 = mybir.dt.float8_e4m3fn_x4
-ACT = mybir.ActivationFunctionType
-ALU = mybir.AluOpType
 
 P = 128
 PACK = 4
 ROWS = D // PACK
-NM = 512
-BANK = 512
+NM = 128
+HALF = 512
+UNITS = G * N // HALF
 RUN = 4
 
-X_CHUNKS = [256, 256, 512]
-UNITS = [[0, 0, 512], [1, 0, 512], [2, 0, 512], [3, 0, 512], [0, 512, 512], [1, 512, 512], [2, 512, 512], [3, 512, 512]]
-BANKS_OF = [2, 2, 1, 1]
-PROGRAM = [
-    ["small"],
-    ["ldw1", 0, 128],
-    ["ldx", 0],
-    ["ldx", 1],
-    ["ldb", "s"],
-    ["ldx", 2],
-    ["ldhs", "s"],
-    ["ldw2", 0],
-    ["ldw2", 1],
-    ["cw1", 0, "v", 0, 96],
-    ["cw1", 0, "a", 96, 128],
-    ["cx", 0, "v", 0, 256],
-    ["qw1", 0, 4],
-    ["cx", 1, "a", 160, 256],
-    ["cx", 1, "v", 0, 160],
-    ["qx", 0, 0, 256],
-    ["qx", 1, 0, 256],
-    ["mm1", 0, [0], 0, 512],
-    ["mm1", 0, [1], 0, 512],
-    ["mm1", 1, [0], 0, 512],
-    ["silu", 0, [0], 0, 512],
-    ["cx", 2, "v", 0, 512],
-    ["silu", 0, [1], 0, 512],
-    ["mm1", 0, [2], 0, 512],
-    ["silu", 1, [0], 0, 512],
-    ["mm1", 0, [3], 0, 512],
-    ["mm1", 1, [1], 0, 512],
-    ["silu", 0, [2], 0, 512],
-    ["qx", 2, 0, 512],
-    ["mm1", 1, [2], 0, 512],
-    ["mm1", 2, [0], 0, 512],
-    ["silu", 0, [3], 0, 512],
-    ["silu", 1, [1], 0, 512],
-    ["tt", 0, 0, 512],
-    ["silu", 1, [2], 0, 512],
-    ["mm1", 1, [3], 0, 512],
-    ["mm1", 4, [0], 0, 512],
-    ["silu", 2, [0], 0, 512],
-    ["silu", 1, [3], 0, 512],
-    ["mm1", 2, [1], 0, 512],
-    ["mm1", 4, [1], 0, 512],
-    ["silu", 4, [0], 0, 512],
-    ["cw2", 0, "v"],
-    ["cw2", 1, "v"],
-    ["silu", 2, [1], 0, 512],
-    ["tt", 1, 0, 512],
-    ["mm1", 4, [2], 0, 512],
-    ["silu", 4, [1], 0, 512],
-    ["mm1", 2, [2], 0, 512],
-    ["silu", 4, [2], 0, 512],
-    ["mm1", 4, [3], 0, 512],
-    ["mm1", 3, [0], 0, 512],
-    ["silu", 2, [2], 0, 512],
-    ["qw2", 0],
-    ["silu", 4, [3], 0, 512],
-    ["qh", 0, 0, 512],
-    ["mm1", 2, [3], 0, 512],
-    ["mm1", 5, [0], 0, 512],
-    ["silu", 3, [0], 0, 512],
-    ["tt", 4, 0, 512],
-    ["silu", 2, [3], 0, 512],
-    ["mm1", 3, [1], 0, 512],
-    ["mm1", 5, [1], 0, 512],
-    ["silu", 5, [0], 0, 512],
-    ["silu", 3, [1], 0, 512],
-    ["mm1", 5, [2], 0, 512],
-    ["silu", 5, [1], 0, 512],
-    ["qh", 1, 0, 512],
-    ["mm1", 3, [2], 0, 512],
-    ["tt", 2, 0, 512],
-    ["silu", 5, [2], 0, 512],
-    ["mm1", 5, [3], 0, 512],
-    ["mm1", 6, [0], 0, 512],
-    ["silu", 3, [2], 0, 512],
-    ["silu", 5, [3], 0, 512],
-    ["mm1", 3, [3], 0, 512],
-    ["silu", 6, [0], 0, 512],
-    ["qh", 4, 0, 512],
-    ["cw2", 2, "a"],
-    ["mm1", 6, [1], 0, 512],
-    ["tt", 5, 0, 512],
-    ["silu", 3, [3], 0, 512],
-    ["silu", 6, [1], 0, 512],
-    ["mm1", 7, [0], 0, 512],
-    ["cw2", 3, "a"],
-    ["mm1", 6, [2], 0, 512],
-    ["silu", 7, [0], 0, 512],
-    ["qh", 2, 0, 512],
-    ["mm2", 0, 0, 512, 0],
-    ["silu", 6, [2], 0, 512],
-    ["tt", 3, 0, 512],
-    ["mm1", 7, [1], 0, 512],
-    ["ev", 0, 0, 512, 0, "a"],
-    ["mm1", 6, [3], 0, 512],
-    ["silu", 7, [1], 0, 512],
-    ["mm2", 1, 0, 512, 1],
-    ["st", 0, 0, 512],
-    ["silu", 6, [3], 0, 512],
-    ["mm1", 7, [2], 0, 512],
-    ["qh", 5, 0, 512],
-    ["ev", 1, 0, 512, 1, "a"],
-    ["tt", 6, 0, 512],
-    ["silu", 7, [2], 0, 512],
-    ["st", 1, 0, 512],
-    ["mm1", 7, [3], 0, 512],
-    ["mm2", 4, 0, 512, 0],
-    ["silu", 7, [3], 0, 512],
-    ["qw2", 1],
-    ["ev", 4, 0, 512, 0, "a"],
-    ["qh", 3, 0, 512],
-    ["mm2", 2, 0, 512, 1],
-    ["tt", 7, 0, 256],
-    ["st", 4, 0, 512],
-    ["mm2", 5, 0, 512, 0],
-    ["ev", 2, 0, 512, 1, "a"],
-    ["qh", 6, 0, 512],
-    ["ev", 5, 0, 512, 0, "a"],
-    ["mm2", 3, 0, 512, 1],
-    ["st", 2, 0, 512],
-    ["tt", 7, 256, 512],
-    ["mm2", 6, 0, 512, 0],
-    ["st", 5, 0, 512],
-    ["ev", 3, 0, 512, 1, "a"],
-    ["qh", 7, 0, 256],
-    ["ev", 6, 0, 512, 0, "a"],
-    ["st", 3, 0, 512],
-    ["qh", 7, 256, 512],
-    ["st", 6, 0, 512],
-    ["mm2", 7, 0, 512, 1],
-    ["ev", 7, 0, 256, 1, "a"],
-    ["ev", 7, 256, 512, 1, "a"],
-    ["st", 7, 0, 256],
-    ["st", 7, 256, 512],
-]
+LEAD = NM
+X_LOADS = [(0, LEAD), (LEAD, HALF), (HALF, N)]
+W1_SPLIT = 96
+Z_BANKS = [2, 2, 1, 1]
+Y_BANKS = 2
+SCALAR_ORDER = "0020012132113243453v4465576576w767"
+LAST_PIECES = [(0, 256), (256, 384), (384, 512)]
 
 
 def tile_rows_gmlp_silu_bias_kernel(tc, x, w1, hs, w2, b, out):
@@ -170,138 +38,177 @@ def tile_rows_gmlp_silu_bias_kernel(tc, x, w1, hs, w2, b, out):
         def sb(name, shape, dtype):
             return keep.tile(shape, dtype, name=name, align_bytes=64)
 
-        x_rows = x.rearrange("g (p j) n -> (g p) j n", j=PACK)
-        w1_rows = w1.rearrange("g (p j) k -> (g p) j k", j=PACK)
-        w2_rows = w2.rearrange("g (p j) m -> p g j m", j=PACK)
-
-        x_start = [sum(X_CHUNKS[:i]) for i in range(len(X_CHUNKS))]
-        x_raw = [sb("x_raw%d" % i, [P, PACK, w], F32) for i, w in enumerate(X_CHUNKS)]
-        x_bf = [sb("x_bf%d" % i, [P, w * PACK], BF16) for i, w in enumerate(X_CHUNKS)]
+        x_raw = [sb("x_raw%d" % i, [P, PACK, n1 - n0], F32) for i, (n0, n1) in enumerate(X_LOADS)]
+        x_bf = sb("x_bf", [P, N * PACK], BF16)
         x_codes = sb("x_codes", [P, N], U32)
         x_scales = sb("x_scales", [P, N], U8)
         w1_raw = sb("w1_raw", [P, PACK, K], F32)
         w1_bf = sb("w1_bf", [P, K * PACK], BF16)
         w1_codes = sb("w1_codes", [P, K], U32)
         w1_scales = sb("w1_scales", [P, K], U8)
-        w2_raw = [sb("w2_raw%d" % i, [P, 2, PACK, M], F32) for i in range(2)]
-        w2_bf = [sb("w2_bf%d" % i, [P, 2 * M * PACK], BF16) for i in range(2)]
-        w2_codes = [sb("w2_codes%d" % i, [P, 2 * M], U32) for i in range(2)]
-        w2_scales = [sb("w2_scales%d" % i, [P, 2 * M], U8) for i in range(2)]
-        b_sb = sb("b_sb", [P, G, 8], F32)
-        hs_sb = sb("hs_sb", [P, G, 8], F32)
-        warm = sb("warm", [P, 8], F32)
-        act = {}
-        for step in PROGRAM:
-            if step[0] == "silu" and (step[1], step[3]) not in act:
-                act[(step[1], step[3])] = sb("act%d_%d" % (step[1], step[3]), [P, PACK, step[4] - step[3]], F32)
-        h_bf = [sb("h_bf%d" % u, [P, w * PACK], BF16) for u, (g, n0, w) in enumerate(UNITS)]
-        h_codes = [sb("h_codes%d" % u, [P, w], U32) for u, (g, n0, w) in enumerate(UNITS)]
-        h_scales = [sb("h_scales%d" % u, [P, w], U8) for u, (g, n0, w) in enumerate(UNITS)]
-        res = [sb("res%d" % u, [P, w], F32) for u, (g, n0, w) in enumerate(UNITS)]
-        z_banks = [[psum.tile([P, BANK], F32, name="bank_z%d_%d" % (g, i)) for i in range(BANKS_OF[g])] for g in range(G)]
-        y_banks = [psum.tile([P, BANK], F32, name="bank_y%d" % i) for i in range(8 - sum(BANKS_OF))]
+        w2_raw = sb("w2_raw", [P, G, PACK, M], F32)
+        w2_bf = sb("w2_bf", [P, G * M * PACK], BF16)
+        w2_codes = sb("w2_codes", [P, G * M], U32)
+        w2_scales = sb("w2_scales", [P, G * M], U8)
+        b_sb = sb("b_sb", [P, G, 2 * PACK], F32)
+        hs_sb = sb("hs_sb", [P, G, 2 * PACK], F32)
+        warm = sb("warm", [P, 2 * PACK], F32)
+        act = [sb("act%d" % u, [P, PACK, HALF], F32) for u in range(UNITS)]
+        h_bf = [sb("h_bf%d" % u, [P, HALF * PACK], BF16) for u in range(UNITS)]
+        h_codes = [sb("h_codes%d" % u, [P, HALF], U32) for u in range(UNITS)]
+        h_scales = [sb("h_scales%d" % u, [P, HALF], U8) for u in range(UNITS)]
+        result = [sb("result%d" % u, [P, HALF], F32) for u in range(UNITS)]
+        z_banks = [[psum.tile([P, HALF], F32, name="bank_z%d_%d" % (g, i)) for i in range(Z_BANKS[g])] for g in range(G)]
+        y_banks = [psum.tile([P, HALF], F32, name="bank_y%d" % i) for i in range(Y_BANKS)]
+
+        x_rows = x.rearrange("g (p j) n -> (g p) j n", j=PACK)
+        w2_rows = w2.rearrange("g (p j) m -> p g (j m)", j=PACK)
+
+        def load_x(i):
+            nc.sync.dma_start(out=x_raw[i][:], in_=x_rows[:, :, X_LOADS[i][0] : X_LOADS[i][1]])
+
+        def load_w2(g0, g1):
+            nc.sync.dma_start(out=w2_raw[:, g0:g1].rearrange("p g j m -> p g (j m)"), in_=w2_rows[:, g0:g1])
+
+        def load_per_hidden(tile, vec):
+            nc.sync.dma_start(out=tile[:, :, 0:PACK], in_=vec.rearrange("g (s r) o -> s g (r o)", r=PACK))
+
+        nc.vector.memset(warm[:, 0:1], 0.0)
+        nc.scalar.activation(out=warm[:, PACK : PACK + 1], in_=warm[:, 0:1], func=mybir.ActivationFunctionType.Silu)
+
+        nc.sync.dma_start(out=w1_raw[:], in_=w1.rearrange("g (p j) k -> (g p) j k", j=PACK))
+        load_x(0)
+        load_per_hidden(b_sb, b)
+        load_x(1)
+        load_per_hidden(hs_sb, hs)
+        load_w2(0, 2)
+        load_x(2)
+        load_w2(2, G)
+
+        def interleave(copy, dst, src):
+            copy(out=dst.rearrange("p (c i j) -> p c j i", i=RUN, j=PACK), in_=src.rearrange("p j (c i) -> p c j i", i=RUN))
+
+        def quantise(codes, scales, values, c0, c1):
+            nc.vector.quantize_mx(out=codes[:, c0:c1].bitcast(FP8X4), scales=scales[:, c0:c1], in_=values[:, PACK * c0 : PACK * c1])
+
+        def cast_w1(copy, s0, s1):
+            dealt = w1_bf[:].rearrange("p (r s j) -> p s j r", r=PACK, j=PACK)
+            copy(out=dealt[:, s0:s1], in_=w1_raw[:].rearrange("p j (s r) -> p s j r", r=PACK)[:, s0:s1])
+
+        def cast_x(i):
+            interleave(nc.vector.tensor_copy, x_bf[:, PACK * X_LOADS[i][0] : PACK * X_LOADS[i][1]], x_raw[i][:])
+
+        def cast_w2(copy, g):
+            interleave(copy, w2_bf[:, g * M * PACK : (g + 1) * M * PACK], w2_raw[:, g])
+
         fills = [0] * G
-        where = {}
 
-        def copy(eng, out, in_):
-            if eng == "v":
-                nc.vector.tensor_copy(out=out, in_=in_)
-            else:
-                nc.scalar.copy(out=out, in_=in_)
-
-        def quant(codes, scales, src):
-            nc.vector.quantize_mx(out=codes.bitcast(FP8X4), scales=scales, in_=src)
-
-        for step in PROGRAM:
-            kind = step[0]
-            if kind == "ldx":
-                i = step[1]
-                nc.sync.dma_start(out=x_raw[i][:], in_=x_rows[:, :, x_start[i] : x_start[i] + X_CHUNKS[i]])
-            elif kind == "ldw1":
-                s0, s1 = step[1:]
-                nc.sync.dma_start(out=w1_raw[:, :, 4 * s0 : 4 * s1], in_=w1_rows[:, :, 4 * s0 : 4 * s1])
-            elif kind == "ldw2":
-                i = step[1]
-                nc.sync.dma_start(out=w2_raw[i][:].rearrange("p g j m -> p g (j m)"), in_=w2_rows[:, 2 * i : 2 * i + 2].rearrange("p g j m -> p g (j m)"))
-            elif kind == "small":
-                nc.vector.memset(warm[:, 0:1], 0.0)
-                nc.scalar.activation(out=warm[:, 4:5], in_=warm[:, 0:1], func=ACT.Silu)
-            elif kind == "ldb":
-                (nc.sync if step[1] == "s" else nc.scalar).dma_start(out=b_sb[:, :, 0:PACK], in_=b.rearrange("g (p r) o -> p g (r o)", r=PACK))
-            elif kind == "ldhs":
-                (nc.sync if step[1] == "s" else nc.scalar).dma_start(out=hs_sb[:, :, 0:PACK], in_=hs.rearrange("g (p r) o -> p g (r o)", r=PACK))
-            elif kind == "cx":
-                i, eng, c0, c1 = step[1:]
-                copy(eng, x_bf[i][:, PACK * c0 : PACK * c1].rearrange("p (c i j) -> p c j i", i=RUN, j=PACK), x_raw[i][:, :, c0:c1].rearrange("p j (c i) -> p c j i", i=RUN))
-            elif kind == "qx":
-                i, c0, c1 = step[1:]
-                quant(x_codes[:, x_start[i] + c0 : x_start[i] + c1], x_scales[:, x_start[i] + c0 : x_start[i] + c1], x_bf[i][:, PACK * c0 : PACK * c1])
-            elif kind == "cw1":
-                i, eng, s0, s1 = step[1:]
-                dst = w1_bf[:].rearrange("p (r s j) -> p s j r", r=PACK, j=PACK)[:, s0:s1]
-                copy(eng, dst, w1_raw[:].rearrange("p j (s r) -> p s j r", r=PACK)[:, s0:s1])
-            elif kind == "qw1":
-                r0, r1 = step[1:]
-                quant(w1_codes[:, r0 * P : r1 * P], w1_scales[:, r0 * P : r1 * P], w1_bf[:, r0 * P * PACK : r1 * P * PACK])
-            elif kind == "cw2":
-                i, gg, eng = step[1] // 2, step[1] % 2, step[2]
-                dst = w2_bf[i][:, gg * 512 : gg * 512 + 512].rearrange("p (c i j) -> p c j i", i=RUN, j=PACK)
-                copy(eng, dst, w2_raw[i][:, gg].rearrange("p j (c i) -> p c j i", i=RUN))
-            elif kind == "qw2":
-                i = step[1]
-                quant(w2_codes[i][:], w2_scales[i][:], w2_bf[i][:])
-            elif kind == "mm1":
-                u, rs, c0, c1 = step[1:]
-                g, n0, w = UNITS[u]
-                n0, w = n0 + c0, c1 - c0
-                bank = z_banks[g][fills[g] % BANKS_OF[g]]
-                fills[g] += 1
-                rows = slice(ROWS * g, ROWS * g + ROWS)
-                for a, r in enumerate(rs):
-                    where[(u, r, c0)] = bank[:, a * w : a * w + w]
-                    for c in range(0, w, NM):
-                        o = n0 + c
-                        nc.tensor.matmul_mx(
-                            out=bank[:, a * w + c : a * w + c + NM],
-                            lhsT=w1_codes[rows, r * P : r * P + P].bitcast(FP8X4),
-                            lhsT_scale=w1_scales[rows, r * P : r * P + P],
-                            rhs=x_codes[rows, o : o + NM].bitcast(FP8X4),
-                            rhs_scale=x_scales[rows, o : o + NM],
-                            start=True, stop=True)
-            elif kind == "silu":
-                u, rs, c0, c1 = step[1:]
-                g, n0, w = UNITS[u]
-                for r in rs:
-                    nc.scalar.activation(out=act[(u, c0)][:, r, :], in_=where[(u, r, c0)], func=ACT.Silu, bias=b_sb[:, g, r : r + 1])
-            elif kind == "tt":
-                u, c0, c1 = step[1:]
-                g, n0, w = UNITS[u]
-                a0 = max(c for (v, c) in act if v == u and c <= c0)
-                nc.vector.tensor_tensor(
-                    out=h_bf[u][:, PACK * c0 : PACK * c1].rearrange("p (c i r) -> p c r i", i=RUN, r=PACK),
-                    in0=act[(u, a0)][:, :, c0 - a0 : c1 - a0].rearrange("p r (c i) -> p c r i", i=RUN),
-                    in1=hs_sb[:, g, 0:PACK].unsqueeze(1).unsqueeze(3).to_broadcast([P, (c1 - c0) // RUN, PACK, RUN]),
-                    op=ALU.mult)
-            elif kind == "qh":
-                u, c0, c1 = step[1:]
-                quant(h_codes[u][:, c0:c1], h_scales[u][:, c0:c1], h_bf[u][:, PACK * c0 : PACK * c1])
-            elif kind == "mm2":
-                u, c0, c1, bk = step[1:]
-                g, n0, w = UNITS[u]
-                wc = slice((g % 2) * M, (g % 2) * M + M)
-                for c in range(c0, c1, NM):
+        def first_layer(u, rs, c0, c1):
+            g, n0, width = u % G, HALF * (u // G) + c0, c1 - c0
+            bank = z_banks[g][fills[g] % Z_BANKS[g]]
+            fills[g] += 1
+            rows = slice(ROWS * g, ROWS * (g + 1))
+            for place, r in enumerate(rs):
+                for c in range(0, width, NM):
                     nc.tensor.matmul_mx(
-                        out=y_banks[bk][:, c : c + NM],
-                        lhsT=w2_codes[g // 2][:, wc].bitcast(FP8X4),
-                        lhsT_scale=w2_scales[g // 2][:, wc],
-                        rhs=h_codes[u][:, c : c + NM].bitcast(FP8X4),
-                        rhs_scale=h_scales[u][:, c : c + NM],
-                        start=True, stop=True)
-            elif kind == "ev":
-                u, c0, c1, bk, eng = step[1:]
-                g, n0, w = UNITS[u]
-                copy(eng, res[u][:, c0:c1], y_banks[bk][:, c0:c1])
-            elif kind == "st":
-                u, c0, c1 = step[1:]
-                g, n0, w = UNITS[u]
-                nc.sync.dma_start(out=out[g, :, n0 + c0 : n0 + c1], in_=res[u][:, c0:c1])
+                        out=bank[:, place * width + c : place * width + c + NM],
+                        lhsT=w1_codes[rows, r * P : (r + 1) * P].bitcast(FP8X4),
+                        lhsT_scale=w1_scales[rows, r * P : (r + 1) * P],
+                        rhs=x_codes[rows, n0 + c : n0 + c + NM].bitcast(FP8X4),
+                        rhs_scale=x_scales[rows, n0 + c : n0 + c + NM],
+                        start=True,
+                        stop=True,
+                    )
+            for place, r in enumerate(rs):
+                nc.scalar.activation(
+                    out=act[u][:, r, c0:c1],
+                    in_=bank[:, place * width : (place + 1) * width],
+                    func=mybir.ActivationFunctionType.Silu,
+                    bias=b_sb[:, g, r : r + 1],
+                )
+
+        def scale_h(u, c0, c1):
+            nc.vector.tensor_tensor(
+                out=h_bf[u][:, PACK * c0 : PACK * c1].rearrange("p (c i r) -> p c r i", i=RUN, r=PACK),
+                in0=act[u][:, :, c0:c1].rearrange("p r (c i) -> p c r i", i=RUN),
+                in1=hs_sb[:, u % G, 0:PACK].unsqueeze(1).unsqueeze(3).to_broadcast([P, (c1 - c0) // RUN, PACK, RUN]),
+                op=mybir.AluOpType.mult,
+            )
+
+        def quantise_h(u, c0, c1):
+            quantise(h_codes[u], h_scales[u], h_bf[u], c0, c1)
+
+        def second_layer(u, c0, c1, bank, copy):
+            g, n0 = u % G, HALF * (u // G)
+            for c in range(c0, c1, NM):
+                nc.tensor.matmul_mx(
+                    out=bank[:, c : c + NM],
+                    lhsT=w2_codes[:, g * M : (g + 1) * M].bitcast(FP8X4),
+                    lhsT_scale=w2_scales[:, g * M : (g + 1) * M],
+                    rhs=h_codes[u][:, c : c + NM].bitcast(FP8X4),
+                    rhs_scale=h_scales[u][:, c : c + NM],
+                    start=True,
+                    stop=True,
+                )
+            copy(out=result[u][:, c0:c1], in_=bank[:, c0:c1])
+            nc.sync.dma_start(out=out[g, :, n0 + c0 : n0 + c1], in_=result[u][:, c0:c1])
+
+        cast_w1(nc.vector.tensor_copy, 0, W1_SPLIT)
+        cast_w1(nc.scalar.copy, W1_SPLIT, P)
+        cast_x(0)
+        quantise(w1_codes, w1_scales, w1_bf, 0, K // 2)
+        quantise(x_codes, x_scales, x_bf, 0, LEAD)
+        quantise(w1_codes, w1_scales, w1_bf, K // 2, K)
+        cast_x(1)
+        quantise(x_codes, x_scales, x_bf, LEAD, 2 * LEAD)
+        quantise(x_codes, x_scales, x_bf, 2 * LEAD, HALF)
+        cast_w2(nc.vector.tensor_copy, 0)
+
+        first_layer(0, [0, 1], 0, LEAD)
+        first_layer(0, [2, 3], 0, LEAD)
+        scale_h(0, 0, LEAD)
+        for g in range(1, G):
+            first_layer(g, range(PACK), 0, LEAD)
+            scale_h(g, 0, LEAD)
+        cast_x(2)
+
+        last = UNITS - 1
+
+        def after_unit(u):
+            scale_h(u, LEAD if u < G else 0, HALF)
+            if u == 0:
+                quantise(x_codes, x_scales, x_bf, HALF, N)
+                cast_w2(nc.vector.tensor_copy, 1)
+                quantise_h(0, 0, HALF)
+            elif u == 1:
+                quantise(w2_codes, w2_scales, w2_bf, 0, 2 * M)
+            else:
+                if u == 5:
+                    quantise(w2_codes, w2_scales, w2_bf, 2 * M, G * M)
+                quantise_h(u - 1, 0, HALF)
+
+        next_r = [0] * UNITS
+        for step in SCALAR_ORDER:
+            if step == "v":
+                cast_w2(nc.scalar.copy, 2)
+            elif step == "w":
+                cast_w2(nc.scalar.copy, 3)
+                after_unit(5)
+            else:
+                u = int(step)
+                first_layer(u, [next_r[u]], LEAD if u < G else 0, HALF)
+                next_r[u] += 1
+                if next_r[u] == PACK and u not in (5, last):
+                    after_unit(u)
+
+        waiting = (last - 1, 0, HALF)
+        for c0, c1 in LAST_PIECES:
+            scale_h(last, c0, c1)
+            quantise_h(*waiting)
+            waiting = (last, c0, c1)
+        quantise_h(*waiting)
+
+        pieces = [(u, 0, HALF) for u in range(last)] + [(last, c0, c1) for c0, c1 in LAST_PIECES]
+        for i, (u, c0, c1) in enumerate(pieces):
+            copy = nc.vector.tensor_copy if i == len(pieces) - 1 else nc.scalar.copy
+            second_layer(u, c0, c1, y_banks[i % Y_BANKS], copy)

@@ -20,11 +20,13 @@ UNITS = G * N // HALF
 RUN = 4
 
 LEAD = NM
-X_LOADS = [(0, LEAD), (LEAD, HALF), (HALF, N)]
-W1_SPLIT = 96
-Z_BANKS = [2, 2, 1, 1]
+X_LOADS = [(0, LEAD), (LEAD, 3 * LEAD), (3 * LEAD, HALF), (HALF, N)]
+W1_SPLIT = 88
+Z_BANKS = [2, 1, 2, 1]
 Y_BANKS = 2
-SCALAR_ORDER = "0020012132113243453v4465576576w767"
+W2_ON_VECTOR = 1
+CAST_AFTER = (3,)
+LEADS = 4
 LAST_PIECES = [(0, 256), (256, 384), (384, 512)]
 
 
@@ -81,8 +83,9 @@ def tile_rows_gmlp_silu_bias_kernel(tc, x, w1, hs, w2, b, out):
         load_per_hidden(b_sb, b)
         load_x(1)
         load_per_hidden(hs_sb, hs)
-        load_w2(0, 2)
         load_x(2)
+        load_x(3)
+        load_w2(0, 2)
         load_w2(2, G)
 
         def interleave(copy, dst, src):
@@ -95,8 +98,8 @@ def tile_rows_gmlp_silu_bias_kernel(tc, x, w1, hs, w2, b, out):
             dealt = w1_bf[:].rearrange("p (r s j) -> p s j r", r=PACK, j=PACK)
             copy(out=dealt[:, s0:s1], in_=w1_raw[:].rearrange("p j (s r) -> p s j r", r=PACK)[:, s0:s1])
 
-        def cast_x(i):
-            interleave(nc.vector.tensor_copy, x_bf[:, PACK * X_LOADS[i][0] : PACK * X_LOADS[i][1]], x_raw[i][:])
+        def cast_x(copy, i):
+            interleave(copy, x_bf[:, PACK * X_LOADS[i][0] : PACK * X_LOADS[i][1]], x_raw[i][:])
 
         def cast_w2(copy, g):
             interleave(copy, w2_bf[:, g * M * PACK : (g + 1) * M * PACK], w2_raw[:, g])
@@ -153,54 +156,52 @@ def tile_rows_gmlp_silu_bias_kernel(tc, x, w1, hs, w2, b, out):
             copy(out=result[u][:, c0:c1], in_=bank[:, c0:c1])
             nc.sync.dma_start(out=out[g, :, n0 + c0 : n0 + c1], in_=result[u][:, c0:c1])
 
-        cast_w1(nc.vector.tensor_copy, 0, W1_SPLIT)
-        cast_w1(nc.scalar.copy, W1_SPLIT, P)
-        cast_x(0)
+        on_vector, on_scalar = nc.vector.tensor_copy, nc.scalar.copy
+        cast_w1(on_vector, 0, W1_SPLIT)
+        cast_w1(on_scalar, W1_SPLIT, P)
+        cast_x(on_vector, 0)
         quantise(w1_codes, w1_scales, w1_bf, 0, K // 2)
-        quantise(x_codes, x_scales, x_bf, 0, LEAD)
+        quantise(x_codes, x_scales, x_bf, *X_LOADS[0])
         quantise(w1_codes, w1_scales, w1_bf, K // 2, K)
-        cast_x(1)
-        quantise(x_codes, x_scales, x_bf, LEAD, 2 * LEAD)
-        quantise(x_codes, x_scales, x_bf, 2 * LEAD, HALF)
-        cast_w2(nc.vector.tensor_copy, 0)
+        cast_x(on_vector, 1)
 
         first_layer(0, [0, 1], 0, LEAD)
         first_layer(0, [2, 3], 0, LEAD)
         scale_h(0, 0, LEAD)
-        for g in range(1, G):
+        cast_x(on_vector, 2)
+        quantise(x_codes, x_scales, x_bf, *X_LOADS[1])
+        quantise(x_codes, x_scales, x_bf, *X_LOADS[2])
+        for g in range(1, LEADS):
             first_layer(g, range(PACK), 0, LEAD)
             scale_h(g, 0, LEAD)
-        cast_x(2)
+        cast_x(on_vector, 3)
+        for g in range(W2_ON_VECTOR):
+            cast_w2(on_vector, g)
+        quantise(x_codes, x_scales, x_bf, *X_LOADS[3])
 
         last = UNITS - 1
-
-        def after_unit(u):
-            scale_h(u, LEAD if u < G else 0, HALF)
-            if u == 0:
-                quantise(x_codes, x_scales, x_bf, HALF, N)
-                cast_w2(nc.vector.tensor_copy, 1)
-                quantise_h(0, 0, HALF)
-            elif u == 1:
-                quantise(w2_codes, w2_scales, w2_bf, 0, 2 * M)
+        one_bank = {2 * PACK * (u // 2) - 2 + 3 * r: (u, r) for u in range(1, UNITS, 2) for r in range(PACK)}
+        two_banks = [(u, r) for u in range(0, UNITS, 2) for r in range(PACK)]
+        casts = list(range(W2_ON_VECTOR, G))
+        for place in range(min(one_bank), max(one_bank) + 1):
+            if place in one_bank:
+                u, r = one_bank[place]
+            elif two_banks:
+                u, r = two_banks.pop(0)
             else:
-                if u == 5:
-                    quantise(w2_codes, w2_scales, w2_bf, 2 * M, G * M)
-                quantise_h(u - 1, 0, HALF)
+                cast_w2(on_scalar, casts.pop(0))
+                continue
+            first_layer(u, [r], LEAD if u < LEADS else 0, HALF)
+            if r == PACK - 1 and u != last:
+                for i in range(CAST_AFTER.count(u)):
+                    cast_w2(on_scalar, casts.pop(0))
+                scale_h(u, LEAD if u < LEADS else 0, HALF)
+                if u > 0:
+                    quantise_h(u - 1, 0, HALF)
+                if u == G:
+                    quantise(w2_codes, w2_scales, w2_bf, 0, 2 * M)
 
-        next_r = [0] * UNITS
-        for step in SCALAR_ORDER:
-            if step == "v":
-                cast_w2(nc.scalar.copy, 2)
-            elif step == "w":
-                cast_w2(nc.scalar.copy, 3)
-                after_unit(5)
-            else:
-                u = int(step)
-                first_layer(u, [next_r[u]], LEAD if u < G else 0, HALF)
-                next_r[u] += 1
-                if next_r[u] == PACK and u not in (5, last):
-                    after_unit(u)
-
+        quantise(w2_codes, w2_scales, w2_bf, 2 * M, G * M)
         waiting = (last - 1, 0, HALF)
         for c0, c1 in LAST_PIECES:
             scale_h(last, c0, c1)
@@ -208,7 +209,7 @@ def tile_rows_gmlp_silu_bias_kernel(tc, x, w1, hs, w2, b, out):
             waiting = (last, c0, c1)
         quantise_h(*waiting)
 
-        pieces = [(u, 0, HALF) for u in range(last)] + [(last, c0, c1) for c0, c1 in LAST_PIECES]
+        pieces = [(u, 0, HALF) for u in sorted(range(last), key=lambda u: u % G // 2)] + [(last, c0, c1) for c0, c1 in LAST_PIECES]
         for i, (u, c0, c1) in enumerate(pieces):
-            copy = nc.vector.tensor_copy if i == len(pieces) - 1 else nc.scalar.copy
+            copy = on_vector if i == len(pieces) - 1 else on_scalar
             second_layer(u, c0, c1, y_banks[i % Y_BANKS], copy)

@@ -20,12 +20,11 @@ UNITS = G * N // HALF
 RUN = 4
 
 LEAD = NM
-X_LOADS = [(0, LEAD), (LEAD, 3 * LEAD), (3 * LEAD, HALF), (HALF, N)]
-W1_SPLIT = 88
+X_LOADS = [(0, LEAD), (LEAD, 2 * LEAD), (2 * LEAD, HALF), (HALF, N)]
 Z_BANKS = [2, 1, 2, 1]
 Y_BANKS = 2
-W2_ON_VECTOR = 1
-CAST_AFTER = (3,)
+W2_ON_VECTOR = 2
+CAST_AFTER = ()
 LEADS = 4
 LAST_PIECES = [(0, 256), (256, 384), (384, 512)]
 
@@ -82,11 +81,11 @@ def tile_rows_gmlp_silu_bias_kernel(tc, x, w1, hs, w2, b, out):
         load_x(0)
         load_per_hidden(b_sb, b)
         load_x(1)
-        load_per_hidden(hs_sb, hs)
+        load_w2(0, 1)
         load_x(2)
+        load_per_hidden(hs_sb, hs)
         load_x(3)
-        load_w2(0, 2)
-        load_w2(2, G)
+        load_w2(1, G)
 
         def interleave(copy, dst, src):
             copy(out=dst.rearrange("p (c i j) -> p c j i", i=RUN, j=PACK), in_=src.rearrange("p j (c i) -> p c j i", i=RUN))
@@ -94,9 +93,9 @@ def tile_rows_gmlp_silu_bias_kernel(tc, x, w1, hs, w2, b, out):
         def quantise(codes, scales, values, c0, c1):
             nc.vector.quantize_mx(out=codes[:, c0:c1].bitcast(FP8X4), scales=scales[:, c0:c1], in_=values[:, PACK * c0 : PACK * c1])
 
-        def cast_w1(copy, s0, s1):
+        def cast_w1(copy, r0, r1):
             dealt = w1_bf[:].rearrange("p (r s j) -> p s j r", r=PACK, j=PACK)
-            copy(out=dealt[:, s0:s1], in_=w1_raw[:].rearrange("p j (s r) -> p s j r", r=PACK)[:, s0:s1])
+            copy(out=dealt[:, :, :, r0:r1], in_=w1_raw[:].rearrange("p j (s r) -> p s j r", r=PACK)[:, :, :, r0:r1])
 
         def cast_x(copy, i):
             interleave(copy, x_bf[:, PACK * X_LOADS[i][0] : PACK * X_LOADS[i][1]], x_raw[i][:])
@@ -157,27 +156,28 @@ def tile_rows_gmlp_silu_bias_kernel(tc, x, w1, hs, w2, b, out):
             nc.sync.dma_start(out=out[g, :, n0 + c0 : n0 + c1], in_=result[u][:, c0:c1])
 
         on_vector, on_scalar = nc.vector.tensor_copy, nc.scalar.copy
-        cast_w1(on_vector, 0, W1_SPLIT)
-        cast_w1(on_scalar, W1_SPLIT, P)
+        cast_w1(on_vector, 0, 2)
+        cast_w1(on_scalar, 2, PACK)
         cast_x(on_vector, 0)
+        cast_x(on_scalar, 1)
         quantise(w1_codes, w1_scales, w1_bf, 0, K // 2)
         quantise(x_codes, x_scales, x_bf, *X_LOADS[0])
         quantise(w1_codes, w1_scales, w1_bf, K // 2, K)
-        cast_x(on_vector, 1)
+        cast_w2(on_vector, 0)
+        quantise(x_codes, x_scales, x_bf, *X_LOADS[1])
+        cast_x(on_vector, 2)
 
         first_layer(0, [0, 1], 0, LEAD)
         first_layer(0, [2, 3], 0, LEAD)
         scale_h(0, 0, LEAD)
-        cast_x(on_vector, 2)
-        quantise(x_codes, x_scales, x_bf, *X_LOADS[1])
         quantise(x_codes, x_scales, x_bf, *X_LOADS[2])
         for g in range(1, LEADS):
             first_layer(g, range(PACK), 0, LEAD)
             scale_h(g, 0, LEAD)
         cast_x(on_vector, 3)
-        for g in range(W2_ON_VECTOR):
-            cast_w2(on_vector, g)
+        cast_w2(on_vector, 1)
         quantise(x_codes, x_scales, x_bf, *X_LOADS[3])
+        quantise(w2_codes, w2_scales, w2_bf, 0, 2 * M)
 
         last = UNITS - 1
         one_bank = {2 * PACK * (u // 2) - 2 + 3 * r: (u, r) for u in range(1, UNITS, 2) for r in range(PACK)}
@@ -198,8 +198,7 @@ def tile_rows_gmlp_silu_bias_kernel(tc, x, w1, hs, w2, b, out):
                 scale_h(u, LEAD if u < LEADS else 0, HALF)
                 if u > 0:
                     quantise_h(u - 1, 0, HALF)
-                if u == G:
-                    quantise(w2_codes, w2_scales, w2_bf, 0, 2 * M)
+
 
         quantise(w2_codes, w2_scales, w2_bf, 2 * M, G * M)
         waiting = (last - 1, 0, HALF)

@@ -20,7 +20,7 @@ UNITS = G * N // HALF
 RUN = 4
 
 LEAD = NM
-X_LOADS = [(0, LEAD), (LEAD, 2 * LEAD), (2 * LEAD, HALF), (HALF, N)]
+X_LOADS = [(0, LEAD), (LEAD, HALF), (HALF, N)]
 Z_BANKS = [2, 1, 2, 1]
 Y_BANKS = 2
 W2_ON_VECTOR = 2
@@ -81,11 +81,10 @@ def tile_rows_gmlp_silu_bias_kernel(tc, x, w1, hs, w2, b, out):
         load_x(0)
         load_per_hidden(b_sb, b)
         load_x(1)
-        load_w2(0, 1)
-        load_x(2)
         load_per_hidden(hs_sb, hs)
-        load_x(3)
-        load_w2(1, G)
+        load_w2(0, 2)
+        load_x(2)
+        load_w2(2, G)
 
         def interleave(copy, dst, src):
             copy(out=dst.rearrange("p (c i j) -> p c j i", i=RUN, j=PACK), in_=src.rearrange("p j (c i) -> p c j i", i=RUN))
@@ -159,25 +158,24 @@ def tile_rows_gmlp_silu_bias_kernel(tc, x, w1, hs, w2, b, out):
         cast_w1(on_vector, 0, 2)
         cast_w1(on_scalar, 2, PACK)
         cast_x(on_vector, 0)
-        cast_x(on_scalar, 1)
         quantise(w1_codes, w1_scales, w1_bf, 0, K // 2)
         quantise(x_codes, x_scales, x_bf, *X_LOADS[0])
         quantise(w1_codes, w1_scales, w1_bf, K // 2, K)
-        cast_w2(on_vector, 0)
-        quantise(x_codes, x_scales, x_bf, *X_LOADS[1])
-        cast_x(on_vector, 2)
+        cast_x(on_vector, 1)
 
         first_layer(0, [0, 1], 0, LEAD)
         first_layer(0, [2, 3], 0, LEAD)
         scale_h(0, 0, LEAD)
-        quantise(x_codes, x_scales, x_bf, *X_LOADS[2])
+        quantise(x_codes, x_scales, x_bf, LEAD, 2 * LEAD)
+        quantise(x_codes, x_scales, x_bf, 2 * LEAD, HALF)
         for g in range(1, LEADS):
             first_layer(g, range(PACK), 0, LEAD)
+            if g == LEADS - 1:
+                for i in range(W2_ON_VECTOR):
+                    cast_w2(on_vector, i)
+                cast_x(on_vector, 2)
             scale_h(g, 0, LEAD)
-        cast_x(on_vector, 3)
-        cast_w2(on_vector, 1)
-        quantise(x_codes, x_scales, x_bf, *X_LOADS[3])
-        quantise(w2_codes, w2_scales, w2_bf, 0, 2 * M)
+        quantise(x_codes, x_scales, x_bf, *X_LOADS[2])
 
         last = UNITS - 1
         one_bank = {2 * PACK * (u // 2) - 2 + 3 * r: (u, r) for u in range(1, UNITS, 2) for r in range(PACK)}
@@ -198,15 +196,17 @@ def tile_rows_gmlp_silu_bias_kernel(tc, x, w1, hs, w2, b, out):
                 scale_h(u, LEAD if u < LEADS else 0, HALF)
                 if u > 0:
                     quantise_h(u - 1, 0, HALF)
+                else:
+                    quantise(w2_codes, w2_scales, w2_bf, 0, 2 * M)
 
 
         quantise(w2_codes, w2_scales, w2_bf, 2 * M, G * M)
-        waiting = (last - 1, 0, HALF)
-        for c0, c1 in LAST_PIECES:
+        quantise_h(last - 1, 0, HALF)
+        for i, (c0, c1) in enumerate(LAST_PIECES):
             scale_h(last, c0, c1)
-            quantise_h(*waiting)
-            waiting = (last, c0, c1)
-        quantise_h(*waiting)
+            if i > 0:
+                quantise_h(last, *LAST_PIECES[i - 1])
+        quantise_h(last, *LAST_PIECES[-1])
 
         pieces = [(u, 0, HALF) for u in sorted(range(last), key=lambda u: u % G // 2)] + [(last, c0, c1) for c0, c1 in LAST_PIECES]
         for i, (u, c0, c1) in enumerate(pieces):

@@ -53,7 +53,6 @@ def tile_rows_gmlp_silu_bias_kernel(tc, x, w1, hs, w2, b, out):
         w2_scales = sb("w2_scales", [P, G * M], U8)
         b_sb = sb("b_sb", [P, G, 2 * PACK], F32)
         hs_sb = sb("hs_sb", [P, G, 2 * PACK], F32)
-        warm = sb("warm", [P, 2 * PACK], F32)
         act = [sb("act%d" % u, [P, PACK, HALF], F32) for u in range(UNITS)]
         h_bf = [sb("h_bf%d" % u, [P, HALF * PACK], BF16) for u in range(UNITS)]
         h_codes = [sb("h_codes%d" % u, [P, HALF], U32) for u in range(UNITS)]
@@ -74,16 +73,13 @@ def tile_rows_gmlp_silu_bias_kernel(tc, x, w1, hs, w2, b, out):
         def load_per_hidden(tile, vec):
             nc.sync.dma_start(out=tile[:, :, 0:PACK], in_=vec.rearrange("g (s r) o -> s g (r o)", r=PACK))
 
-        nc.vector.memset(warm[:, 0:1], 0.0)
-        nc.scalar.activation(out=warm[:, PACK : PACK + 1], in_=warm[:, 0:1], func=mybir.ActivationFunctionType.Silu)
-
         nc.sync.dma_start(out=w1_raw[:], in_=w1.rearrange("g (p j) k -> (g p) j k", j=PACK))
         load_x(0)
         load_per_hidden(b_sb, b)
         load_x(1)
         load_per_hidden(hs_sb, hs)
-        load_w2(0, 2)
         load_x(2)
+        load_w2(0, 2)
         load_w2(2, G)
 
         def interleave(copy, dst, src):
@@ -170,11 +166,10 @@ def tile_rows_gmlp_silu_bias_kernel(tc, x, w1, hs, w2, b, out):
         quantise(x_codes, x_scales, x_bf, 2 * LEAD, HALF)
         for g in range(1, LEADS):
             first_layer(g, range(PACK), 0, LEAD)
-            if g == LEADS - 1:
-                for i in range(W2_ON_VECTOR):
-                    cast_w2(on_vector, i)
-                cast_x(on_vector, 2)
             scale_h(g, 0, LEAD)
+        cast_x(on_vector, 2)
+        for g in range(W2_ON_VECTOR):
+            cast_w2(on_vector, g)
         quantise(x_codes, x_scales, x_bf, *X_LOADS[2])
 
         last = UNITS - 1

@@ -23,9 +23,6 @@ LEAD = NM
 X_LOADS = [(0, LEAD), (LEAD, HALF), (HALF, N)]
 Z_BANKS = [2, 1, 2, 1]
 Y_BANKS = 2
-W2_ON_VECTOR = 2
-CAST_AFTER = ()
-LEADS = 4
 LAST_PIECES = [(0, 256), (256, 384), (384, 512)]
 
 
@@ -54,9 +51,9 @@ def tile_rows_gmlp_silu_bias_kernel(tc, x, w1, hs, w2, b, out):
         b_sb = sb("b_sb", [P, G, 2 * PACK], F32)
         hs_sb = sb("hs_sb", [P, G, 2 * PACK], F32)
         act = [sb("act%d" % u, [P, PACK, HALF], F32) for u in range(UNITS)]
-        h_bf = [sb("h_bf%d" % u, [P, HALF * PACK], BF16) for u in range(UNITS)]
-        h_codes = [sb("h_codes%d" % u, [P, HALF], U32) for u in range(UNITS)]
-        h_scales = [sb("h_scales%d" % u, [P, HALF], U8) for u in range(UNITS)]
+        h_bf = sb("h_bf", [P, G * N * PACK], BF16)
+        h_codes = sb("h_codes", [P, G * N], U32)
+        h_scales = sb("h_scales", [P, G * N], U8)
         result = [sb("result%d" % u, [P, HALF], F32) for u in range(UNITS)]
         z_banks = [[psum.tile([P, HALF], F32, name="bank_z%d_%d" % (g, i)) for i in range(Z_BANKS[g])] for g in range(G)]
         y_banks = [psum.tile([P, HALF], F32, name="bank_y%d" % i) for i in range(Y_BANKS)]
@@ -92,8 +89,8 @@ def tile_rows_gmlp_silu_bias_kernel(tc, x, w1, hs, w2, b, out):
             dealt = w1_bf[:].rearrange("p (r s j) -> p s j r", r=PACK, j=PACK)
             copy(out=dealt[:, :, :, r0:r1], in_=w1_raw[:].rearrange("p j (s r) -> p s j r", r=PACK)[:, :, :, r0:r1])
 
-        def cast_x(copy, i):
-            interleave(copy, x_bf[:, PACK * X_LOADS[i][0] : PACK * X_LOADS[i][1]], x_raw[i][:])
+        def cast_x(copy, i, n0, n1):
+            interleave(copy, x_bf[:, PACK * n0 : PACK * n1], x_raw[i][:, :, n0 - X_LOADS[i][0] : n1 - X_LOADS[i][0]])
 
         def cast_w2(copy, g):
             interleave(copy, w2_bf[:, g * M * PACK : (g + 1) * M * PACK], w2_raw[:, g])
@@ -124,16 +121,24 @@ def tile_rows_gmlp_silu_bias_kernel(tc, x, w1, hs, w2, b, out):
                     bias=b_sb[:, g, r : r + 1],
                 )
 
+        def word_of(u, c):
+            if u >= G:
+                return u * HALF + c
+            return u * LEAD + c if c < LEAD else G * LEAD + u * (HALF - LEAD) + c - LEAD
+
         def scale_h(u, c0, c1):
             nc.vector.tensor_tensor(
-                out=h_bf[u][:, PACK * c0 : PACK * c1].rearrange("p (c i r) -> p c r i", i=RUN, r=PACK),
+                out=h_bf[:, PACK * word_of(u, c0) : PACK * (word_of(u, c0) + c1 - c0)].rearrange("p (c i r) -> p c r i", i=RUN, r=PACK),
                 in0=act[u][:, :, c0:c1].rearrange("p r (c i) -> p c r i", i=RUN),
                 in1=hs_sb[:, u % G, 0:PACK].unsqueeze(1).unsqueeze(3).to_broadcast([P, (c1 - c0) // RUN, PACK, RUN]),
                 op=mybir.AluOpType.mult,
             )
 
         def quantise_h(u, c0, c1):
-            quantise(h_codes[u], h_scales[u], h_bf[u], c0, c1)
+            quantise(h_codes, h_scales, h_bf, word_of(u, c0), word_of(u, c0) + c1 - c0)
+
+        def quantise_first(w0, w1):
+            quantise(h_codes, h_scales, h_bf, w0, w1)
 
         def second_layer(u, c0, c1, bank, copy):
             g, n0 = u % G, HALF * (u // G)
@@ -142,8 +147,8 @@ def tile_rows_gmlp_silu_bias_kernel(tc, x, w1, hs, w2, b, out):
                     out=bank[:, c : c + NM],
                     lhsT=w2_codes[:, g * M : (g + 1) * M].bitcast(FP8X4),
                     lhsT_scale=w2_scales[:, g * M : (g + 1) * M],
-                    rhs=h_codes[u][:, c : c + NM].bitcast(FP8X4),
-                    rhs_scale=h_scales[u][:, c : c + NM],
+                    rhs=h_codes[:, word_of(u, c) : word_of(u, c) + NM].bitcast(FP8X4),
+                    rhs_scale=h_scales[:, word_of(u, c) : word_of(u, c) + NM],
                     start=True,
                     stop=True,
                 )
@@ -151,59 +156,79 @@ def tile_rows_gmlp_silu_bias_kernel(tc, x, w1, hs, w2, b, out):
             nc.sync.dma_start(out=out[g, :, n0 + c0 : n0 + c1], in_=result[u][:, c0:c1])
 
         on_vector, on_scalar = nc.vector.tensor_copy, nc.scalar.copy
+        warm_in, warm_out = sb("warm_in", [P, 1], F32), sb("warm_out", [P, 1], F32)
+        nc.gpsimd.memset(warm_in[:], 0.0)
+        nc.scalar.activation(out=warm_out[:], in_=warm_in[:], func=mybir.ActivationFunctionType.Silu)
         cast_w1(on_vector, 0, 2)
         cast_w1(on_scalar, 2, PACK)
-        cast_x(on_vector, 0)
+        cast_x(on_vector, 0, 0, LEAD)
         quantise(w1_codes, w1_scales, w1_bf, 0, K // 2)
-        quantise(x_codes, x_scales, x_bf, *X_LOADS[0])
+        quantise(x_codes, x_scales, x_bf, 0, LEAD)
         quantise(w1_codes, w1_scales, w1_bf, K // 2, K)
-        cast_x(on_vector, 1)
+        cast_x(on_vector, 1, 2 * LEAD, HALF)
+        cast_x(on_vector, 1, LEAD, 2 * LEAD)
+        quantise(x_codes, x_scales, x_bf, 2 * LEAD, HALF)
+        quantise(x_codes, x_scales, x_bf, LEAD, 2 * LEAD)
 
         first_layer(0, [0, 1], 0, LEAD)
         first_layer(0, [2, 3], 0, LEAD)
         scale_h(0, 0, LEAD)
-        quantise(x_codes, x_scales, x_bf, LEAD, 2 * LEAD)
-        quantise(x_codes, x_scales, x_bf, 2 * LEAD, HALF)
-        for g in range(1, LEADS):
+        for g in range(1, G):
             first_layer(g, range(PACK), 0, LEAD)
             scale_h(g, 0, LEAD)
-        cast_x(on_vector, 2)
-        for g in range(W2_ON_VECTOR):
-            cast_w2(on_vector, g)
-        quantise(x_codes, x_scales, x_bf, *X_LOADS[2])
+        cast_x(on_vector, 2, HALF, N)
+        quantise_first(0, 2 * LEAD)
+        quantise(x_codes, x_scales, x_bf, HALF, N)
 
-        last = UNITS - 1
-        one_bank = {2 * PACK * (u // 2) - 2 + 3 * r: (u, r) for u in range(1, UNITS, 2) for r in range(PACK)}
+        def quantise_w2(g0, g1):
+            quantise(w2_codes, w2_scales, w2_bf, g0 * M, g1 * M)
+
+        last = 6
+        one_bank = {start + 3 * r: (u, r) for u, start in ((1, -2), (3, 6), (5, 14), (7, 21)) for r in range(PACK)}
         two_banks = [(u, r) for u in range(0, UNITS, 2) for r in range(PACK)]
-        casts = list(range(W2_ON_VECTOR, G))
-        for place in range(min(one_bank), max(one_bank) + 1):
-            if place in one_bank:
-                u, r = one_bank[place]
-            elif two_banks:
-                u, r = two_banks.pop(0)
-            else:
-                cast_w2(on_scalar, casts.pop(0))
+        casts = {22: 0, 25: 1}
+        for place in range(min(one_bank), min(one_bank) + PACK * UNITS + len(casts)):
+            if place in casts:
+                cast_w2(on_scalar, casts[place])
                 continue
-            first_layer(u, [r], LEAD if u < LEADS else 0, HALF)
-            if r == PACK - 1 and u != last:
-                for i in range(CAST_AFTER.count(u)):
-                    cast_w2(on_scalar, casts.pop(0))
-                scale_h(u, LEAD if u < LEADS else 0, HALF)
-                if u > 0:
+            u, r = one_bank[place] if place in one_bank else two_banks.pop(0)
+            first_layer(u, [r], LEAD if u < G else 0, HALF)
+            if r == PACK - 1 and u < last:
+                scale_h(u, LEAD if u < G else 0, HALF)
+                if u == 0:
+                    quantise_first(2 * LEAD, G * LEAD)
+                elif 2 <= u <= G:
+                    quantise_first((u - 1) * HALF, u * HALF)
+                elif u > G:
                     quantise_h(u - 1, 0, HALF)
-                else:
-                    quantise(w2_codes, w2_scales, w2_bf, 0, 2 * M)
 
+        banks_used = []
 
-        quantise(w2_codes, w2_scales, w2_bf, 2 * M, G * M)
-        quantise_h(last - 1, 0, HALF)
-        for i, (c0, c1) in enumerate(LAST_PIECES):
-            scale_h(last, c0, c1)
-            if i > 0:
-                quantise_h(last, *LAST_PIECES[i - 1])
-        quantise_h(last, *LAST_PIECES[-1])
+        def result_of(u, c0, c1, copy):
+            second_layer(u, c0, c1, y_banks[len(banks_used) % Y_BANKS], copy)
+            banks_used.append(u)
 
-        pieces = [(u, 0, HALF) for u in sorted(range(last), key=lambda u: u % G // 2)] + [(last, c0, c1) for c0, c1 in LAST_PIECES]
-        for i, (u, c0, c1) in enumerate(pieces):
-            copy = on_vector if i == len(pieces) - 1 else on_scalar
-            second_layer(u, c0, c1, y_banks[i % Y_BANKS], copy)
+        quantise_w2(0, 2)
+        quantise_h(5, 0, HALF)
+        scale_h(7, 0, HALF)
+        result_of(0, 0, HALF, on_scalar)
+        result_of(1, 0, HALF, on_scalar)
+        cast_w2(on_scalar, 3)
+        result_of(4, 0, HALF, on_scalar)
+        result_of(5, 0, HALF, on_scalar)
+        cast_w2(on_scalar, 2)
+        quantise_w2(3, 4)
+        quantise_h(7, 0, HALF)
+        scale_h(last, *LAST_PIECES[0])
+        quantise_w2(2, 3)
+        result_of(3, 0, HALF, on_scalar)
+        result_of(7, 0, HALF, on_scalar)
+        result_of(2, 0, HALF, on_scalar)
+        scale_h(last, *LAST_PIECES[1])
+        quantise_h(last, *LAST_PIECES[0])
+        scale_h(last, *LAST_PIECES[2])
+        quantise_h(last, *LAST_PIECES[1])
+        quantise_h(last, *LAST_PIECES[2])
+        result_of(last, *LAST_PIECES[0], on_scalar)
+        result_of(last, *LAST_PIECES[1], on_scalar)
+        result_of(last, *LAST_PIECES[2], on_vector)

@@ -48,8 +48,10 @@ def tile_rows_gmlp_silu_bias_kernel(tc, x, w1, hs, w2, b, out):
         w2_bf = sb("w2_bf", [P, G * M * PACK], BF16)
         w2_codes = sb("w2_codes", [P, G * M], U32)
         w2_scales = sb("w2_scales", [P, G * M], U8)
-        b_sb = sb("b_sb", [P, G, 2 * PACK], F32)
-        hs_sb = sb("hs_sb", [P, G, 2 * PACK], F32)
+        rows_raw = sb("rows_raw", [P, P], F32)
+        rows_dealt = sb("rows_dealt", [P, P], F32)
+        turned = sb("turned", [P, P], F32)
+        hs_sb = sb("hs_sb", [P, G, PACK], F32)
         act = [sb("act%d" % u, [P, PACK, HALF], F32) for u in range(UNITS)]
         h_bf = sb("h_bf", [P, G * N * PACK], BF16)
         h_codes = sb("h_codes", [P, G * N], U32)
@@ -67,14 +69,15 @@ def tile_rows_gmlp_silu_bias_kernel(tc, x, w1, hs, w2, b, out):
         def load_w2(g0, g1):
             nc.sync.dma_start(out=w2_raw[:, g0:g1].rearrange("p g j m -> p g (j m)"), in_=w2_rows[:, g0:g1])
 
-        def load_per_hidden(tile, vec):
-            nc.sync.dma_start(out=tile[:, :, 0:PACK], in_=vec.rearrange("g (s r) o -> s g (r o)", r=PACK))
+        def load_rows(e, vec):
+            nc.sync.dma_start(out=rows_raw[e:P:8, :], in_=vec.rearrange("g (q c) o -> q g (c o)", c=P))
 
+        nc.gpsimd.memset(rows_raw[:], 0.0)
         nc.sync.dma_start(out=w1_raw[:], in_=w1.rearrange("g (p j) k -> (g p) j k", j=PACK))
+        load_rows(0, b)
+        load_rows(1, hs)
         load_x(0)
-        load_per_hidden(b_sb, b)
         load_x(1)
-        load_per_hidden(hs_sb, hs)
         load_x(2)
         load_w2(0, 2)
         load_w2(2, G)
@@ -94,6 +97,15 @@ def tile_rows_gmlp_silu_bias_kernel(tc, x, w1, hs, w2, b, out):
 
         def cast_w2(copy, g):
             interleave(copy, w2_bf[:, g * M * PACK : (g + 1) * M * PACK], w2_raw[:, g])
+
+        def deal_rows():
+            nc.vector.tensor_copy(out=rows_dealt[:].rearrange("p (r c) -> p c r", r=PACK), in_=rows_raw[:].rearrange("p (c r) -> p c r", r=PACK))
+
+        def turn_rows():
+            nc.vector.transpose(out=turned[:], in_=rows_dealt[:])
+
+        def gather_hs():
+            nc.vector.tensor_copy(out=hs_sb[:], in_=turned[:].rearrange("p (r g e) -> p g r e", r=PACK, g=G)[:, :, :, 1])
 
         fills = [0] * G
 
@@ -118,7 +130,7 @@ def tile_rows_gmlp_silu_bias_kernel(tc, x, w1, hs, w2, b, out):
                     out=act[u][:, r, c0:c1],
                     in_=bank[:, place * width : (place + 1) * width],
                     func=mybir.ActivationFunctionType.Silu,
-                    bias=b_sb[:, g, r : r + 1],
+                    bias=turned[:, ROWS * r + 8 * g : ROWS * r + 8 * g + 1],
                 )
 
         def word_of(u, c):
@@ -164,7 +176,10 @@ def tile_rows_gmlp_silu_bias_kernel(tc, x, w1, hs, w2, b, out):
         cast_x(on_vector, 0, 0, LEAD)
         quantise(w1_codes, w1_scales, w1_bf, 0, K // 2)
         quantise(x_codes, x_scales, x_bf, 0, LEAD)
+        deal_rows()
         quantise(w1_codes, w1_scales, w1_bf, K // 2, K)
+        turn_rows()
+        gather_hs()
         cast_x(on_vector, 1, 2 * LEAD, HALF)
         cast_x(on_vector, 1, LEAD, 2 * LEAD)
         quantise(x_codes, x_scales, x_bf, 2 * LEAD, HALF)
@@ -179,24 +194,28 @@ def tile_rows_gmlp_silu_bias_kernel(tc, x, w1, hs, w2, b, out):
         cast_x(on_vector, 2, HALF, N)
         quantise_first(0, 2 * LEAD)
         quantise(x_codes, x_scales, x_bf, HALF, N)
+        cast_w2(on_vector, 0)
 
         def quantise_w2(g0, g1):
             quantise(w2_codes, w2_scales, w2_bf, g0 * M, g1 * M)
 
-        last = 6
-        one_bank = {start + 3 * r: (u, r) for u, start in ((1, -2), (3, 6), (5, 14), (7, 21)) for r in range(PACK)}
+        last = 7
+        one_bank = {start + 3 * r: (u, r) for u, start in ((1, -2), (3, 6), (5, 14), (7, 22)) for r in range(PACK)}
         two_banks = [(u, r) for u in range(0, UNITS, 2) for r in range(PACK)]
-        casts = {22: 0, 25: 1}
+        casts = {29: 2, 30: 3}
         for place in range(min(one_bank), min(one_bank) + PACK * UNITS + len(casts)):
             if place in casts:
                 cast_w2(on_scalar, casts[place])
                 continue
             u, r = one_bank[place] if place in one_bank else two_banks.pop(0)
             first_layer(u, [r], LEAD if u < G else 0, HALF)
-            if r == PACK - 1 and u < last:
+            if r == PACK - 1 and u < 6:
                 scale_h(u, LEAD if u < G else 0, HALF)
                 if u == 0:
+                    cast_w2(on_vector, 1)
                     quantise_first(2 * LEAD, G * LEAD)
+                elif u == 1:
+                    quantise_w2(0, 2)
                 elif 2 <= u <= G:
                     quantise_first((u - 1) * HALF, u * HALF)
                 elif u > G:
@@ -208,22 +227,18 @@ def tile_rows_gmlp_silu_bias_kernel(tc, x, w1, hs, w2, b, out):
             second_layer(u, c0, c1, y_banks[len(banks_used) % Y_BANKS], copy)
             banks_used.append(u)
 
-        quantise_w2(0, 2)
         quantise_h(5, 0, HALF)
-        scale_h(7, 0, HALF)
+        scale_h(6, 0, HALF)
         result_of(0, 0, HALF, on_scalar)
         result_of(1, 0, HALF, on_scalar)
-        cast_w2(on_scalar, 3)
         result_of(4, 0, HALF, on_scalar)
         result_of(5, 0, HALF, on_scalar)
-        cast_w2(on_scalar, 2)
-        quantise_w2(3, 4)
-        quantise_h(7, 0, HALF)
+        quantise_w2(2, 4)
+        quantise_h(6, 0, HALF)
         scale_h(last, *LAST_PIECES[0])
-        quantise_w2(2, 3)
-        result_of(3, 0, HALF, on_scalar)
-        result_of(7, 0, HALF, on_scalar)
         result_of(2, 0, HALF, on_scalar)
+        result_of(6, 0, HALF, on_scalar)
+        result_of(3, 0, HALF, on_scalar)
         scale_h(last, *LAST_PIECES[1])
         quantise_h(last, *LAST_PIECES[0])
         scale_h(last, *LAST_PIECES[2])

@@ -17,7 +17,7 @@ ROWS = D // PACK
 NM = 128
 HALF = 512
 UNITS = G * N // HALF
-RUN = 4
+RUN = 2
 
 LEAD = NM
 X_LOADS = [(0, LEAD), (LEAD, HALF), (HALF, N)]
@@ -74,9 +74,9 @@ def tile_rows_gmlp_silu_bias_kernel(tc, x, w1, hs, w2, b, out):
 
         nc.gpsimd.memset(rows_raw[:], 0.0)
         nc.sync.dma_start(out=w1_raw[:], in_=w1.rearrange("g (p j) k -> (g p) j k", j=PACK))
+        load_x(0)
         load_rows(0, b)
         load_rows(1, hs)
-        load_x(0)
         load_x(1)
         load_x(2)
         load_w2(0, 2)
@@ -200,10 +200,10 @@ def tile_rows_gmlp_silu_bias_kernel(tc, x, w1, hs, w2, b, out):
             quantise(w2_codes, w2_scales, w2_bf, g0 * M, g1 * M)
 
         last = 7
-        one_bank = {start + 3 * r: (u, r) for u, start in ((1, -2), (3, 6), (5, 14), (7, 22)) for r in range(PACK)}
+        one_bank = {start + 3 * r: (u, r) for u, start in ((1, -2), (3, 6), (5, 14), (7, 21)) for r in range(PACK)}
         two_banks = [(u, r) for u in range(0, UNITS, 2) for r in range(PACK)]
-        casts = {29: 2, 30: 3}
-        for place in range(min(one_bank), min(one_bank) + PACK * UNITS + len(casts)):
+        casts = {29: 2}
+        for place in range(min(one_bank), 31):
             if place in casts:
                 cast_w2(on_scalar, casts[place])
                 continue
@@ -230,6 +230,7 @@ def tile_rows_gmlp_silu_bias_kernel(tc, x, w1, hs, w2, b, out):
         quantise_h(5, 0, HALF)
         scale_h(6, 0, HALF)
         result_of(0, 0, HALF, on_scalar)
+        cast_w2(on_scalar, 3)
         result_of(1, 0, HALF, on_scalar)
         result_of(4, 0, HALF, on_scalar)
         result_of(5, 0, HALF, on_scalar)
@@ -237,8 +238,8 @@ def tile_rows_gmlp_silu_bias_kernel(tc, x, w1, hs, w2, b, out):
         quantise_h(6, 0, HALF)
         scale_h(last, *LAST_PIECES[0])
         result_of(2, 0, HALF, on_scalar)
-        result_of(6, 0, HALF, on_scalar)
         result_of(3, 0, HALF, on_scalar)
+        result_of(6, 0, HALF, on_scalar)
         scale_h(last, *LAST_PIECES[1])
         quantise_h(last, *LAST_PIECES[0])
         scale_h(last, *LAST_PIECES[2])

@@ -14,15 +14,18 @@ FP8X4 = mybir.dt.float8_e4m3fn_x4
 P = 128
 PACK = 4
 ROWS = D // PACK
+QUAD = 32
 NM = 128
 HALF = 512
 UNITS = G * N // HALF
 RUN = 2
 
 LEAD = NM
-X_LOADS = [(0, LEAD), (LEAD, HALF), (HALF, N)]
+X_LOADS = [(0, LEAD), (LEAD, 3 * LEAD), (3 * LEAD, HALF), (HALF, N)]
 Z_BANKS = [2, 1, 2, 1]
 Y_BANKS = 2
+BANK_PERIOD = 3
+W2_SPLIT = 2
 LAST_PIECES = [(0, 256), (256, 384), (384, 512)]
 
 
@@ -48,9 +51,10 @@ def tile_rows_gmlp_silu_bias_kernel(tc, x, w1, hs, w2, b, out):
         w2_bf = sb("w2_bf", [P, G * M * PACK], BF16)
         w2_codes = sb("w2_codes", [P, G * M], U32)
         w2_scales = sb("w2_scales", [P, G * M], U8)
-        rows_raw = sb("rows_raw", [P, P], F32)
-        rows_dealt = sb("rows_dealt", [P, P], F32)
-        turned = sb("turned", [P, P], F32)
+        pitch = P // (G * G)
+        vec_rows = sb("vec_rows", [P, P], F32)
+        vec_dealt = sb("vec_dealt", [P, P], F32)
+        vec_turned = sb("vec_turned", [P, P], F32)
         hs_sb = sb("hs_sb", [P, G, PACK], F32)
         act = [sb("act%d" % u, [P, PACK, HALF], F32) for u in range(UNITS)]
         h_bf = sb("h_bf", [P, G * N * PACK], BF16)
@@ -66,21 +70,17 @@ def tile_rows_gmlp_silu_bias_kernel(tc, x, w1, hs, w2, b, out):
         def load_x(i):
             nc.sync.dma_start(out=x_raw[i][:], in_=x_rows[:, :, X_LOADS[i][0] : X_LOADS[i][1]])
 
-        def load_w2(g0, g1):
-            nc.sync.dma_start(out=w2_raw[:, g0:g1].rearrange("p g j m -> p g (j m)"), in_=w2_rows[:, g0:g1])
-
-        def load_rows(e, vec):
-            nc.sync.dma_start(out=rows_raw[e:P:8, :], in_=vec.rearrange("g (q c) o -> q g (c o)", c=P))
-
-        nc.gpsimd.memset(rows_raw[:], 0.0)
+        nc.gpsimd.memset(vec_rows[:], 0.0)
         nc.sync.dma_start(out=w1_raw[:], in_=w1.rearrange("g (p j) k -> (g p) j k", j=PACK))
         load_x(0)
-        load_rows(0, b)
-        load_rows(1, hs)
-        load_x(1)
-        load_x(2)
-        load_w2(0, 2)
-        load_w2(2, G)
+        for e, vec in enumerate((b, hs)):
+            nc.sync.dma_start(out=vec_rows[e:P:pitch, :], in_=vec.rearrange("g (q i) o -> q g (i o)", i=P))
+        for i in range(1, len(X_LOADS)):
+            load_x(i)
+        for g0, g1 in ((0, W2_SPLIT), (W2_SPLIT, G)):
+            nc.sync.dma_start(out=w2_raw[:, g0:g1].rearrange("p g j m -> p g (j m)"), in_=w2_rows[:, g0:g1])
+
+        on_vector, on_scalar = nc.vector.tensor_copy, nc.scalar.copy
 
         def interleave(copy, dst, src):
             copy(out=dst.rearrange("p (c i j) -> p c j i", i=RUN, j=PACK), in_=src.rearrange("p j (c i) -> p c j i", i=RUN))
@@ -88,24 +88,25 @@ def tile_rows_gmlp_silu_bias_kernel(tc, x, w1, hs, w2, b, out):
         def quantise(codes, scales, values, c0, c1):
             nc.vector.quantize_mx(out=codes[:, c0:c1].bitcast(FP8X4), scales=scales[:, c0:c1], in_=values[:, PACK * c0 : PACK * c1])
 
-        def cast_w1(copy, r0, r1):
+        def cast_w1(copy, r0, r1, s0, s1):
             dealt = w1_bf[:].rearrange("p (r s j) -> p s j r", r=PACK, j=PACK)
-            copy(out=dealt[:, :, :, r0:r1], in_=w1_raw[:].rearrange("p j (s r) -> p s j r", r=PACK)[:, :, :, r0:r1])
+            raw = w1_raw[:].rearrange("p j (s r) -> p s j r", r=PACK)
+            copy(out=dealt[:, s0:s1, :, r0:r1], in_=raw[:, s0:s1, :, r0:r1])
 
-        def cast_x(copy, i, n0, n1):
-            interleave(copy, x_bf[:, PACK * n0 : PACK * n1], x_raw[i][:, :, n0 - X_LOADS[i][0] : n1 - X_LOADS[i][0]])
+        def quantise_w1(r0, r1):
+            quantise(w1_codes, w1_scales, w1_bf, r0 * P, r1 * P)
+
+        def cast_x(i):
+            interleave(on_vector, x_bf[:, PACK * X_LOADS[i][0] : PACK * X_LOADS[i][1]], x_raw[i][:])
+
+        def quantise_x(i):
+            quantise(x_codes, x_scales, x_bf, *X_LOADS[i])
 
         def cast_w2(copy, g):
             interleave(copy, w2_bf[:, g * M * PACK : (g + 1) * M * PACK], w2_raw[:, g])
 
-        def deal_rows():
-            nc.vector.tensor_copy(out=rows_dealt[:].rearrange("p (r c) -> p c r", r=PACK), in_=rows_raw[:].rearrange("p (c r) -> p c r", r=PACK))
-
-        def turn_rows():
-            nc.vector.transpose(out=turned[:], in_=rows_dealt[:])
-
-        def gather_hs():
-            nc.vector.tensor_copy(out=hs_sb[:], in_=turned[:].rearrange("p (r g e) -> p g r e", r=PACK, g=G)[:, :, :, 1])
+        def quantise_w2(g0, g1):
+            quantise(w2_codes, w2_scales, w2_bf, g0 * M, g1 * M)
 
         fills = [0] * G
 
@@ -114,10 +115,10 @@ def tile_rows_gmlp_silu_bias_kernel(tc, x, w1, hs, w2, b, out):
             bank = z_banks[g][fills[g] % Z_BANKS[g]]
             fills[g] += 1
             rows = slice(ROWS * g, ROWS * (g + 1))
-            for place, r in enumerate(rs):
+            for slot, r in enumerate(rs):
                 for c in range(0, width, NM):
                     nc.tensor.matmul_mx(
-                        out=bank[:, place * width + c : place * width + c + NM],
+                        out=bank[:, slot * width + c : slot * width + c + NM],
                         lhsT=w1_codes[rows, r * P : (r + 1) * P].bitcast(FP8X4),
                         lhsT_scale=w1_scales[rows, r * P : (r + 1) * P],
                         rhs=x_codes[rows, n0 + c : n0 + c + NM].bitcast(FP8X4),
@@ -125,12 +126,13 @@ def tile_rows_gmlp_silu_bias_kernel(tc, x, w1, hs, w2, b, out):
                         start=True,
                         stop=True,
                     )
-            for place, r in enumerate(rs):
+            for slot, r in enumerate(rs):
+                b_column = QUAD * r + pitch * g
                 nc.scalar.activation(
                     out=act[u][:, r, c0:c1],
-                    in_=bank[:, place * width : (place + 1) * width],
+                    in_=bank[:, slot * width : (slot + 1) * width],
                     func=mybir.ActivationFunctionType.Silu,
-                    bias=turned[:, ROWS * r + 8 * g : ROWS * r + 8 * g + 1],
+                    bias=vec_turned[:, b_column : b_column + 1],
                 )
 
         def word_of(u, c):
@@ -139,112 +141,96 @@ def tile_rows_gmlp_silu_bias_kernel(tc, x, w1, hs, w2, b, out):
             return u * LEAD + c if c < LEAD else G * LEAD + u * (HALF - LEAD) + c - LEAD
 
         def scale_h(u, c0, c1):
+            w0 = word_of(u, c0)
             nc.vector.tensor_tensor(
-                out=h_bf[:, PACK * word_of(u, c0) : PACK * (word_of(u, c0) + c1 - c0)].rearrange("p (c i r) -> p c r i", i=RUN, r=PACK),
+                out=h_bf[:, PACK * w0 : PACK * (w0 + c1 - c0)].rearrange("p (c i r) -> p c r i", i=RUN, r=PACK),
                 in0=act[u][:, :, c0:c1].rearrange("p r (c i) -> p c r i", i=RUN),
-                in1=hs_sb[:, u % G, 0:PACK].unsqueeze(1).unsqueeze(3).to_broadcast([P, (c1 - c0) // RUN, PACK, RUN]),
+                in1=hs_sb[:, u % G].unsqueeze(1).unsqueeze(3).to_broadcast([P, (c1 - c0) // RUN, PACK, RUN]),
                 op=mybir.AluOpType.mult,
             )
 
-        def quantise_h(u, c0, c1):
-            quantise(h_codes, h_scales, h_bf, word_of(u, c0), word_of(u, c0) + c1 - c0)
+        def quantise_h(w0, w1_end):
+            quantise(h_codes, h_scales, h_bf, w0, w1_end)
 
-        def quantise_first(w0, w1):
-            quantise(h_codes, h_scales, h_bf, w0, w1)
+        results_made = []
 
-        def second_layer(u, c0, c1, bank, copy):
+        def second_layer(u, c0, c1, copy):
             g, n0 = u % G, HALF * (u // G)
+            bank = y_banks[len(results_made) % Y_BANKS]
+            results_made.append(u)
             for c in range(c0, c1, NM):
+                w0 = word_of(u, c)
                 nc.tensor.matmul_mx(
                     out=bank[:, c : c + NM],
                     lhsT=w2_codes[:, g * M : (g + 1) * M].bitcast(FP8X4),
                     lhsT_scale=w2_scales[:, g * M : (g + 1) * M],
-                    rhs=h_codes[:, word_of(u, c) : word_of(u, c) + NM].bitcast(FP8X4),
-                    rhs_scale=h_scales[:, word_of(u, c) : word_of(u, c) + NM],
+                    rhs=h_codes[:, w0 : w0 + NM].bitcast(FP8X4),
+                    rhs_scale=h_scales[:, w0 : w0 + NM],
                     start=True,
                     stop=True,
                 )
             copy(out=result[u][:, c0:c1], in_=bank[:, c0:c1])
             nc.sync.dma_start(out=out[g, :, n0 + c0 : n0 + c1], in_=result[u][:, c0:c1])
 
-        on_vector, on_scalar = nc.vector.tensor_copy, nc.scalar.copy
-        warm_in, warm_out = sb("warm_in", [P, 1], F32), sb("warm_out", [P, 1], F32)
-        nc.gpsimd.memset(warm_in[:], 0.0)
-        nc.scalar.activation(out=warm_out[:], in_=warm_in[:], func=mybir.ActivationFunctionType.Silu)
-        cast_w1(on_vector, 0, 2)
-        cast_w1(on_scalar, 2, PACK)
-        cast_x(on_vector, 0, 0, LEAD)
-        quantise(w1_codes, w1_scales, w1_bf, 0, K // 2)
-        quantise(x_codes, x_scales, x_bf, 0, LEAD)
-        deal_rows()
-        quantise(w1_codes, w1_scales, w1_bf, K // 2, K)
-        turn_rows()
-        gather_hs()
-        cast_x(on_vector, 1, 2 * LEAD, HALF)
-        cast_x(on_vector, 1, LEAD, 2 * LEAD)
-        quantise(x_codes, x_scales, x_bf, 2 * LEAD, HALF)
-        quantise(x_codes, x_scales, x_bf, LEAD, 2 * LEAD)
+        cast_w1(on_vector, 0, 2, 0, P)
+        cast_w1(on_scalar, 2, PACK, 0, P // 2)
+        cast_w1(on_vector, 2, PACK, P // 2, P)
+        cast_x(0)
+        on_vector(out=vec_dealt[:].rearrange("p (r c) -> p c r", r=PACK), in_=vec_rows[:].rearrange("p (c r) -> p c r", r=PACK))
+        quantise_w1(0, 2)
+        nc.vector.transpose(out=vec_turned[:], in_=vec_dealt[:])
+        quantise_x(0)
+        quantise_w1(2, PACK)
+        cast_x(1)
+        on_vector(out=hs_sb[:], in_=vec_turned[:].rearrange("p (r g e) -> p g r e", r=PACK, g=G)[:, :, :, 1])
+        quantise_x(1)
+        cast_x(2)
 
         first_layer(0, [0, 1], 0, LEAD)
         first_layer(0, [2, 3], 0, LEAD)
         scale_h(0, 0, LEAD)
+        quantise_x(2)
         for g in range(1, G):
             first_layer(g, range(PACK), 0, LEAD)
+            if g == G - 1:
+                quantise_h(0, 2 * LEAD)
             scale_h(g, 0, LEAD)
-        cast_x(on_vector, 2, HALF, N)
-        quantise_first(0, 2 * LEAD)
-        quantise(x_codes, x_scales, x_bf, HALF, N)
+        cast_x(3)
+        quantise_h(2 * LEAD, G * LEAD)
+        quantise_x(3)
         cast_w2(on_vector, 0)
 
-        def quantise_w2(g0, g1):
-            quantise(w2_codes, w2_scales, w2_bf, g0 * M, g1 * M)
-
-        last = 7
-        one_bank = {start + 3 * r: (u, r) for u, start in ((1, -2), (3, 6), (5, 14), (7, 21)) for r in range(PACK)}
+        last = UNITS - 1
+        one_bank = {PACK * (u - 1) - (u == last) + BANK_PERIOD * r: (u, r) for u in range(1, UNITS, 2) for r in range(PACK)}
         two_banks = [(u, r) for u in range(0, UNITS, 2) for r in range(PACK)]
-        casts = {29: 2}
-        for place in range(min(one_bank), 31):
-            if place in casts:
-                cast_w2(on_scalar, casts[place])
+        for place in range(max(one_bank) + 1):
+            if place not in one_bank and not two_banks:
+                cast_w2(on_scalar, W2_SPLIT)
                 continue
             u, r = one_bank[place] if place in one_bank else two_banks.pop(0)
             first_layer(u, [r], LEAD if u < G else 0, HALF)
-            if r == PACK - 1 and u < 6:
+            if r == PACK - 1 and u < last - 1:
                 scale_h(u, LEAD if u < G else 0, HALF)
                 if u == 0:
                     cast_w2(on_vector, 1)
-                    quantise_first(2 * LEAD, G * LEAD)
                 elif u == 1:
-                    quantise_w2(0, 2)
-                elif 2 <= u <= G:
-                    quantise_first((u - 1) * HALF, u * HALF)
-                elif u > G:
-                    quantise_h(u - 1, 0, HALF)
+                    quantise_w2(0, W2_SPLIT)
+                else:
+                    quantise_h((u - 1) * HALF, u * HALF)
 
-        banks_used = []
-
-        def result_of(u, c0, c1, copy):
-            second_layer(u, c0, c1, y_banks[len(banks_used) % Y_BANKS], copy)
-            banks_used.append(u)
-
-        quantise_h(5, 0, HALF)
-        scale_h(6, 0, HALF)
-        result_of(0, 0, HALF, on_scalar)
-        cast_w2(on_scalar, 3)
-        result_of(1, 0, HALF, on_scalar)
-        result_of(4, 0, HALF, on_scalar)
-        result_of(5, 0, HALF, on_scalar)
-        quantise_w2(2, 4)
-        quantise_h(6, 0, HALF)
-        scale_h(last, *LAST_PIECES[0])
-        result_of(2, 0, HALF, on_scalar)
-        result_of(3, 0, HALF, on_scalar)
-        result_of(6, 0, HALF, on_scalar)
-        scale_h(last, *LAST_PIECES[1])
-        quantise_h(last, *LAST_PIECES[0])
-        scale_h(last, *LAST_PIECES[2])
-        quantise_h(last, *LAST_PIECES[1])
-        quantise_h(last, *LAST_PIECES[2])
-        result_of(last, *LAST_PIECES[0], on_scalar)
-        result_of(last, *LAST_PIECES[1], on_scalar)
-        result_of(last, *LAST_PIECES[2], on_vector)
+        quantise_h((last - 2) * HALF, (last - 1) * HALF)
+        scale_h(last - 1, 0, HALF)
+        second_layer(0, 0, HALF, on_scalar)
+        cast_w2(on_scalar, G - 1)
+        quantise_w2(W2_SPLIT, G)
+        quantise_h((last - 1) * HALF, last * HALF)
+        for i, (c0, c1) in enumerate(LAST_PIECES):
+            scale_h(last, c0, c1)
+            if i > 0:
+                quantise_h(*(word_of(last, c) for c in LAST_PIECES[i - 1]))
+        quantise_h(*(word_of(last, c) for c in LAST_PIECES[-1]))
+        for u in sorted(range(1, last), key=lambda u: u % G >= W2_SPLIT):
+            second_layer(u, 0, HALF, on_scalar)
+        for c0, c1 in LAST_PIECES[:-1]:
+            second_layer(last, c0, c1, on_scalar)
+        second_layer(last, *LAST_PIECES[-1], on_vector)

@@ -25,7 +25,7 @@ X_LOADS = [(0, LEAD), (LEAD, 3 * LEAD), (3 * LEAD, HALF), (HALF, N)]
 Z_BANKS = [2, 1, 2, 1]
 Y_BANKS = 2
 BANK_PERIOD = 3
-W2_SPLIT = 2
+W2_SPLIT = 3
 LAST_PIECES = [(0, 256), (256, 384), (384, 512)]
 
 
@@ -77,7 +77,7 @@ def tile_rows_gmlp_silu_bias_kernel(tc, x, w1, hs, w2, b, out):
             nc.sync.dma_start(out=vec_rows[e:P:pitch, :], in_=vec.rearrange("g (q i) o -> q g (i o)", i=P))
         for i in range(1, len(X_LOADS)):
             load_x(i)
-        for g0, g1 in ((0, W2_SPLIT), (W2_SPLIT, G)):
+        for g0, g1 in ((0, 2), (2, G)):
             nc.sync.dma_start(out=w2_raw[:, g0:g1].rearrange("p g j m -> p g (j m)"), in_=w2_rows[:, g0:g1])
 
         on_vector, on_scalar = nc.vector.tensor_copy, nc.scalar.copy
@@ -208,28 +208,30 @@ def tile_rows_gmlp_silu_bias_kernel(tc, x, w1, hs, w2, b, out):
                 cast_w2(on_scalar, W2_SPLIT)
                 continue
             u, r = one_bank[place] if place in one_bank else two_banks.pop(0)
+            if (u, r) == (last, PACK - 1):
+                for early in range(Y_BANKS):
+                    second_layer(early, 0, HALF, on_scalar)
             first_layer(u, [r], LEAD if u < G else 0, HALF)
             if r == PACK - 1 and u < last - 1:
                 scale_h(u, LEAD if u < G else 0, HALF)
                 if u == 0:
                     cast_w2(on_vector, 1)
                 elif u == 1:
-                    quantise_w2(0, W2_SPLIT)
+                    quantise_w2(0, 2)
+                    cast_w2(on_vector, 2)
                 else:
                     quantise_h((u - 1) * HALF, u * HALF)
 
         quantise_h((last - 2) * HALF, (last - 1) * HALF)
         scale_h(last - 1, 0, HALF)
-        second_layer(0, 0, HALF, on_scalar)
-        cast_w2(on_scalar, G - 1)
-        quantise_w2(W2_SPLIT, G)
+        quantise_w2(2, G)
         quantise_h((last - 1) * HALF, last * HALF)
         for i, (c0, c1) in enumerate(LAST_PIECES):
             scale_h(last, c0, c1)
             if i > 0:
                 quantise_h(*(word_of(last, c) for c in LAST_PIECES[i - 1]))
         quantise_h(*(word_of(last, c) for c in LAST_PIECES[-1]))
-        for u in sorted(range(1, last), key=lambda u: u % G >= W2_SPLIT):
+        for u in sorted(range(Y_BANKS, last), key=lambda u: u % G >= 2):
             second_layer(u, 0, HALF, on_scalar)
         for c0, c1 in LAST_PIECES[:-1]:
             second_layer(last, c0, c1, on_scalar)

@@ -25,7 +25,7 @@ X_LOADS = [(0, LEAD), (LEAD, 3 * LEAD), (3 * LEAD, HALF), (HALF, N)]
 Z_BANKS = [2, 1, 2, 1]
 Y_BANKS = 2
 BANK_PERIOD = 3
-W2_SPLIT = 3
+W2_SPLIT = 2
 LAST_PIECES = [(0, 256), (256, 384), (384, 512)]
 
 
@@ -102,15 +102,18 @@ def tile_rows_gmlp_silu_bias_kernel(tc, x, w1, hs, w2, b, out):
         def quantise_x(i):
             quantise(x_codes, x_scales, x_bf, *X_LOADS[i])
 
-        def cast_w2(copy, g):
-            interleave(copy, w2_bf[:, g * M * PACK : (g + 1) * M * PACK], w2_raw[:, g])
+        def cast_w2(copy, g0, g1):
+            copy(
+                out=w2_bf[:, g0 * M * PACK : g1 * M * PACK].rearrange("p (g c i j) -> p g c j i", g=g1 - g0, i=RUN, j=PACK),
+                in_=w2_raw[:, g0:g1].rearrange("p g j (c i) -> p g c j i", i=RUN),
+            )
 
         def quantise_w2(g0, g1):
             quantise(w2_codes, w2_scales, w2_bf, g0 * M, g1 * M)
 
         fills = [0] * G
 
-        def first_layer(u, rs, c0, c1):
+        def first_layer(u, rs, c0, c1, between=lambda: None):
             g, n0, width = u % G, HALF * (u // G) + c0, c1 - c0
             bank = z_banks[g][fills[g] % Z_BANKS[g]]
             fills[g] += 1
@@ -126,6 +129,7 @@ def tile_rows_gmlp_silu_bias_kernel(tc, x, w1, hs, w2, b, out):
                         start=True,
                         stop=True,
                     )
+            between()
             for slot, r in enumerate(rs):
                 b_column = QUAD * r + pitch * g
                 nc.scalar.activation(
@@ -198,29 +202,27 @@ def tile_rows_gmlp_silu_bias_kernel(tc, x, w1, hs, w2, b, out):
         cast_x(3)
         quantise_h(2 * LEAD, G * LEAD)
         quantise_x(3)
-        cast_w2(on_vector, 0)
+        cast_w2(on_vector, 0, W2_SPLIT)
 
         last = UNITS - 1
         one_bank = {PACK * (u - 1) - (u == last) + BANK_PERIOD * r: (u, r) for u in range(1, UNITS, 2) for r in range(PACK)}
         two_banks = [(u, r) for u in range(0, UNITS, 2) for r in range(PACK)]
         for place in range(max(one_bank) + 1):
             if place not in one_bank and not two_banks:
-                cast_w2(on_scalar, W2_SPLIT)
+                cast_w2(on_scalar, W2_SPLIT, G)
                 continue
             u, r = one_bank[place] if place in one_bank else two_banks.pop(0)
             if (u, r) == (last, PACK - 1):
-                for early in range(Y_BANKS):
-                    second_layer(early, 0, HALF, on_scalar)
+                first_layer(u, [r], 0, HALF, lambda: [second_layer(early, 0, HALF, on_scalar) for early in range(Y_BANKS)])
+                continue
             first_layer(u, [r], LEAD if u < G else 0, HALF)
             if r == PACK - 1 and u < last - 1:
                 scale_h(u, LEAD if u < G else 0, HALF)
                 if u == 0:
-                    cast_w2(on_vector, 1)
-                elif u == 1:
-                    quantise_w2(0, 2)
-                    cast_w2(on_vector, 2)
-                else:
-                    quantise_h((u - 1) * HALF, u * HALF)
+                    quantise_w2(0, W2_SPLIT)
+                if u != 1:
+                    done = max(u - 1, 0)
+                    quantise_h(word_of(done, LEAD if done < G else 0), word_of(done, HALF - 1) + 1)
 
         quantise_h((last - 2) * HALF, (last - 1) * HALF)
         scale_h(last - 1, 0, HALF)

@@ -19,6 +19,7 @@ NM = 128
 HALF = 512
 UNITS = G * N // HALF
 RUN = 2
+CAST_RUN = 4
 
 LEAD = NM
 X_LOADS = [(0, LEAD), (LEAD, 3 * LEAD), (3 * LEAD, HALF), (HALF, N)]
@@ -77,13 +78,10 @@ def tile_rows_gmlp_silu_bias_kernel(tc, x, w1, hs, w2, b, out):
             nc.sync.dma_start(out=vec_rows[e:P:pitch, :], in_=vec.rearrange("g (q i) o -> q g (i o)", i=P))
         for i in range(1, len(X_LOADS)):
             load_x(i)
-        for g0, g1 in ((0, 2), (2, G)):
+        for g0, g1 in ((0, W2_SPLIT), (W2_SPLIT, G)):
             nc.sync.dma_start(out=w2_raw[:, g0:g1].rearrange("p g j m -> p g (j m)"), in_=w2_rows[:, g0:g1])
 
         on_vector, on_scalar = nc.vector.tensor_copy, nc.scalar.copy
-
-        def interleave(copy, dst, src):
-            copy(out=dst.rearrange("p (c i j) -> p c j i", i=RUN, j=PACK), in_=src.rearrange("p j (c i) -> p c j i", i=RUN))
 
         def quantise(codes, scales, values, c0, c1):
             nc.vector.quantize_mx(out=codes[:, c0:c1].bitcast(FP8X4), scales=scales[:, c0:c1], in_=values[:, PACK * c0 : PACK * c1])
@@ -97,15 +95,19 @@ def tile_rows_gmlp_silu_bias_kernel(tc, x, w1, hs, w2, b, out):
             quantise(w1_codes, w1_scales, w1_bf, r0 * P, r1 * P)
 
         def cast_x(i):
-            interleave(on_vector, x_bf[:, PACK * X_LOADS[i][0] : PACK * X_LOADS[i][1]], x_raw[i][:])
+            n0, n1 = X_LOADS[i]
+            on_vector(
+                out=x_bf[:, PACK * n0 : PACK * n1].rearrange("p (c i j) -> p c j i", i=CAST_RUN, j=PACK),
+                in_=x_raw[i][:].rearrange("p j (c i) -> p c j i", i=CAST_RUN),
+            )
 
         def quantise_x(i):
             quantise(x_codes, x_scales, x_bf, *X_LOADS[i])
 
         def cast_w2(copy, g0, g1):
             copy(
-                out=w2_bf[:, g0 * M * PACK : g1 * M * PACK].rearrange("p (g c i j) -> p g c j i", g=g1 - g0, i=RUN, j=PACK),
-                in_=w2_raw[:, g0:g1].rearrange("p g j (c i) -> p g c j i", i=RUN),
+                out=w2_bf[:, g0 * M * PACK : g1 * M * PACK].rearrange("p (g c i j) -> p g c j i", g=g1 - g0, i=CAST_RUN, j=PACK),
+                in_=w2_raw[:, g0:g1].rearrange("p g j (c i) -> p g c j i", i=CAST_RUN),
             )
 
         def quantise_w2(g0, g1):
@@ -113,7 +115,7 @@ def tile_rows_gmlp_silu_bias_kernel(tc, x, w1, hs, w2, b, out):
 
         fills = [0] * G
 
-        def first_layer(u, rs, c0, c1, between=lambda: None):
+        def fill_bank(u, rs, c0, c1):
             g, n0, width = u % G, HALF * (u // G) + c0, c1 - c0
             bank = z_banks[g][fills[g] % Z_BANKS[g]]
             fills[g] += 1
@@ -129,15 +131,24 @@ def tile_rows_gmlp_silu_bias_kernel(tc, x, w1, hs, w2, b, out):
                         start=True,
                         stop=True,
                     )
-            between()
+            return bank
+
+        def empty_bank(bank, u, rs, c0, c1):
+            width = c1 - c0
             for slot, r in enumerate(rs):
-                b_column = QUAD * r + pitch * g
+                b_column = QUAD * r + pitch * (u % G)
                 nc.scalar.activation(
                     out=act[u][:, r, c0:c1],
                     in_=bank[:, slot * width : (slot + 1) * width],
                     func=mybir.ActivationFunctionType.Silu,
                     bias=vec_turned[:, b_column : b_column + 1],
                 )
+
+        def first_layer(u, rs, c0, c1):
+            empty_bank(fill_bank(u, rs, c0, c1), u, rs, c0, c1)
+
+        def after_lead(u):
+            return LEAD if u < G else 0
 
         def word_of(u, c):
             if u >= G:
@@ -155,6 +166,9 @@ def tile_rows_gmlp_silu_bias_kernel(tc, x, w1, hs, w2, b, out):
 
         def quantise_h(w0, w1_end):
             quantise(h_codes, h_scales, h_bf, w0, w1_end)
+
+        def quantise_unit(u):
+            quantise_h(word_of(u, after_lead(u)), word_of(u, HALF - 1) + 1)
 
         results_made = []
 
@@ -207,33 +221,34 @@ def tile_rows_gmlp_silu_bias_kernel(tc, x, w1, hs, w2, b, out):
         last = UNITS - 1
         one_bank = {PACK * (u - 1) - (u == last) + BANK_PERIOD * r: (u, r) for u in range(1, UNITS, 2) for r in range(PACK)}
         two_banks = [(u, r) for u in range(0, UNITS, 2) for r in range(PACK)]
-        for place in range(max(one_bank) + 1):
+        for place in range(max(one_bank)):
             if place not in one_bank and not two_banks:
                 cast_w2(on_scalar, W2_SPLIT, G)
                 continue
             u, r = one_bank[place] if place in one_bank else two_banks.pop(0)
-            if (u, r) == (last, PACK - 1):
-                first_layer(u, [r], 0, HALF, lambda: [second_layer(early, 0, HALF, on_scalar) for early in range(Y_BANKS)])
-                continue
-            first_layer(u, [r], LEAD if u < G else 0, HALF)
+            first_layer(u, [r], after_lead(u), HALF)
             if r == PACK - 1 and u < last - 1:
-                scale_h(u, LEAD if u < G else 0, HALF)
+                scale_h(u, after_lead(u), HALF)
                 if u == 0:
                     quantise_w2(0, W2_SPLIT)
-                if u != 1:
-                    done = max(u - 1, 0)
-                    quantise_h(word_of(done, LEAD if done < G else 0), word_of(done, HALF - 1) + 1)
+                    quantise_unit(0)
+                elif u > 1:
+                    quantise_unit(u - 1)
 
-        quantise_h((last - 2) * HALF, (last - 1) * HALF)
+        last_bank = fill_bank(last, [PACK - 1], 0, HALF)
+        for u in range(Y_BANKS):
+            second_layer(u, 0, HALF, on_scalar)
+        empty_bank(last_bank, last, [PACK - 1], 0, HALF)
+        quantise_unit(last - 2)
         scale_h(last - 1, 0, HALF)
-        quantise_w2(2, G)
-        quantise_h((last - 1) * HALF, last * HALF)
+        quantise_w2(W2_SPLIT, G)
+        quantise_unit(last - 1)
         for i, (c0, c1) in enumerate(LAST_PIECES):
             scale_h(last, c0, c1)
             if i > 0:
                 quantise_h(*(word_of(last, c) for c in LAST_PIECES[i - 1]))
         quantise_h(*(word_of(last, c) for c in LAST_PIECES[-1]))
-        for u in sorted(range(Y_BANKS, last), key=lambda u: u % G >= 2):
+        for u in sorted(range(Y_BANKS, last), key=lambda u: u % G >= W2_SPLIT):
             second_layer(u, 0, HALF, on_scalar)
         for c0, c1 in LAST_PIECES[:-1]:
             second_layer(last, c0, c1, on_scalar)

@@ -25,7 +25,8 @@ LEAD = NM
 X_LOADS = [(0, LEAD), (LEAD, 3 * LEAD), (3 * LEAD, HALF), (HALF, N)]
 Z_BANKS = [2, 1, 2, 1]
 Y_BANKS = 2
-BANK_PERIOD = 3
+BANK_PERIODS = [4, 3]
+ONE_BANK_STARTS = [(0, 3), (0, 7)]
 W2_SPLIT = 2
 LAST_PIECES = [(0, 256), (256, 384), (384, 512)]
 
@@ -61,6 +62,7 @@ def tile_rows_gmlp_silu_bias_kernel(tc, x, w1, hs, w2, b, out):
         h_bf = sb("h_bf", [P, G * N * PACK], BF16)
         h_codes = sb("h_codes", [P, G * N], U32)
         h_scales = sb("h_scales", [P, G * N], U8)
+        h_rows = sb("h_rows", [P, PACK, LAST_PIECES[0][1]], BF16)
         result = [sb("result%d" % u, [P, HALF], F32) for u in range(UNITS)]
         z_banks = [[psum.tile([P, HALF], F32, name="bank_z%d_%d" % (g, i)) for i in range(Z_BANKS[g])] for g in range(G)]
         y_banks = [psum.tile([P, HALF], F32, name="bank_y%d" % i) for i in range(Y_BANKS)]
@@ -164,6 +166,22 @@ def tile_rows_gmlp_silu_bias_kernel(tc, x, w1, hs, w2, b, out):
                 op=mybir.AluOpType.mult,
             )
 
+        def scale_row(r):
+            hs_column = QUAD * r + pitch * ((UNITS - 1) % G) + 1
+            nc.scalar.activation(
+                out=h_rows[:, r, :],
+                in_=act[UNITS - 1][:, r, 0 : LAST_PIECES[0][1]],
+                func=mybir.ActivationFunctionType.Copy,
+                scale=vec_turned[:, hs_column : hs_column + 1],
+            )
+
+        def interleave_rows():
+            w0 = word_of(UNITS - 1, 0)
+            on_vector(
+                out=h_bf[:, PACK * w0 : PACK * (w0 + LAST_PIECES[0][1])].rearrange("p (c i r) -> p c r i", i=CAST_RUN, r=PACK),
+                in_=h_rows[:].rearrange("p r (c i) -> p c r i", i=CAST_RUN),
+            )
+
         def quantise_h(w0, w1_end):
             quantise(h_codes, h_scales, h_bf, w0, w1_end)
 
@@ -219,7 +237,11 @@ def tile_rows_gmlp_silu_bias_kernel(tc, x, w1, hs, w2, b, out):
         cast_w2(on_vector, 0, W2_SPLIT)
 
         last = UNITS - 1
-        one_bank = {PACK * (u - 1) - (u == last) + BANK_PERIOD * r: (u, r) for u in range(1, UNITS, 2) for r in range(PACK)}
+        one_bank = {
+            G * PACK * (u // G) + ONE_BANK_STARTS[u // G][u % G // 2] + BANK_PERIODS[u // G] * r: (u, r)
+            for u in range(1, UNITS, 2)
+            for r in range(PACK)
+        }
         two_banks = [(u, r) for u in range(0, UNITS, 2) for r in range(PACK)]
         for place in range(max(one_bank)):
             if place not in one_bank and not two_banks:
@@ -235,20 +257,24 @@ def tile_rows_gmlp_silu_bias_kernel(tc, x, w1, hs, w2, b, out):
                 elif u > 1:
                     quantise_unit(u - 1)
 
-        last_bank = fill_bank(last, [PACK - 1], 0, HALF)
-        for u in range(Y_BANKS):
-            second_layer(u, 0, HALF, on_scalar)
-        empty_bank(last_bank, last, [PACK - 1], 0, HALF)
+        scale_row(0)
+        first_layer(last, [PACK - 1], 0, HALF)
         quantise_unit(last - 2)
         scale_h(last - 1, 0, HALF)
         quantise_w2(W2_SPLIT, G)
         quantise_unit(last - 1)
-        for i, (c0, c1) in enumerate(LAST_PIECES):
-            scale_h(last, c0, c1)
-            if i > 0:
-                quantise_h(*(word_of(last, c) for c in LAST_PIECES[i - 1]))
+        second_layer(0, 0, HALF, on_scalar)
+        second_layer(1, 0, HALF, on_scalar)
+        scale_row(1)
+        scale_row(2)
+        second_layer(G, 0, HALF, on_scalar)
+        scale_row(3)
+        interleave_rows()
+        for i in range(1, len(LAST_PIECES)):
+            scale_h(last, *LAST_PIECES[i])
+            quantise_h(*(word_of(last, c) for c in LAST_PIECES[i - 1]))
         quantise_h(*(word_of(last, c) for c in LAST_PIECES[-1]))
-        for u in sorted(range(Y_BANKS, last), key=lambda u: u % G >= W2_SPLIT):
+        for u in (G + 1, 2, 3, G + 2):
             second_layer(u, 0, HALF, on_scalar)
         for c0, c1 in LAST_PIECES[:-1]:
             second_layer(last, c0, c1, on_scalar)

@@ -67,13 +67,17 @@ def tile_rows_gmlp_silu_bias_kernel(tc, x, w1, hs, w2, b, out):
         z_banks = [[psum.tile([P, HALF], F32, name="bank_z%d_%d" % (g, i)) for i in range(Z_BANKS[g])] for g in range(G)]
         y_banks = [psum.tile([P, HALF], F32, name="bank_y%d" % i) for i in range(Y_BANKS)]
 
+        idle = sb("idle", [P, 2], F32)
+        nc.vector.memset(idle[:, 0:1], 0.0)
+        nc.scalar.activation(out=idle[:, 1:2], in_=idle[:, 0:1], func=mybir.ActivationFunctionType.Silu)
+
         x_rows = x.rearrange("g (p j) n -> (g p) j n", j=PACK)
         w2_rows = w2.rearrange("g (p j) m -> p g (j m)", j=PACK)
 
         def load_x(i):
             nc.sync.dma_start(out=x_raw[i][:], in_=x_rows[:, :, X_LOADS[i][0] : X_LOADS[i][1]])
 
-        nc.gpsimd.memset(vec_rows[:], 0.0)
+        nc.vector.memset(vec_rows[:], 0.0)
         nc.sync.dma_start(out=w1_raw[:], in_=w1.rearrange("g (p j) k -> (g p) j k", j=PACK))
         load_x(0)
         for e, vec in enumerate((b, hs)):
@@ -96,9 +100,9 @@ def tile_rows_gmlp_silu_bias_kernel(tc, x, w1, hs, w2, b, out):
         def quantise_w1(r0, r1):
             quantise(w1_codes, w1_scales, w1_bf, r0 * P, r1 * P)
 
-        def cast_x(i):
+        def cast_x(i, copy=on_vector):
             n0, n1 = X_LOADS[i]
-            on_vector(
+            copy(
                 out=x_bf[:, PACK * n0 : PACK * n1].rearrange("p (c i j) -> p c j i", i=CAST_RUN, j=PACK),
                 in_=x_raw[i][:].rearrange("p j (c i) -> p c j i", i=CAST_RUN),
             )
@@ -211,12 +215,12 @@ def tile_rows_gmlp_silu_bias_kernel(tc, x, w1, hs, w2, b, out):
         cast_w1(on_vector, 0, 2, 0, P)
         cast_w1(on_scalar, 2, PACK, 0, P // 2)
         cast_w1(on_vector, 2, PACK, P // 2, P)
-        cast_x(0)
-        on_vector(out=vec_dealt[:].rearrange("p (r c) -> p c r", r=PACK), in_=vec_rows[:].rearrange("p (c r) -> p c r", r=PACK))
+        cast_x(0, on_scalar)
+        on_scalar(out=vec_dealt[:].rearrange("p (r c) -> p c r", r=PACK), in_=vec_rows[:].rearrange("p (c r) -> p c r", r=PACK))
         quantise_w1(0, 2)
-        nc.vector.transpose(out=vec_turned[:], in_=vec_dealt[:])
-        quantise_x(0)
         quantise_w1(2, PACK)
+        quantise_x(0)
+        nc.vector.transpose(out=vec_turned[:], in_=vec_dealt[:])
         cast_x(1)
         on_vector(out=hs_sb[:], in_=vec_turned[:].rearrange("p (r g e) -> p g r e", r=PACK, g=G)[:, :, :, 1])
         quantise_x(1)

@@ -23,10 +23,10 @@ CAST_RUN = 4
 
 LEAD = NM
 X_LOADS = [(0, LEAD), (LEAD, 3 * LEAD), (3 * LEAD, HALF), (HALF, N)]
-Z_BANKS = [2, 1, 2, 1]
-Y_BANKS = 2
-BANK_PERIODS = [4, 3]
-ONE_BANK_STARTS = [(0, 3), (0, 7)]
+Z_BANKS = [2, 1, 1, 1]
+Y_BANKS = 3
+REFILL_MARGIN = 512
+PRECEDENCE = [1, 0, 2, 3, 5, 4, 6, 7]
 W2_SPLIT = 2
 LAST_PIECES = [(0, 256), (256, 384), (384, 512)]
 
@@ -241,44 +241,51 @@ def tile_rows_gmlp_silu_bias_kernel(tc, x, w1, hs, w2, b, out):
         cast_w2(on_vector, 0, W2_SPLIT)
 
         last = UNITS - 1
-        one_bank = {
-            G * PACK * (u // G) + ONE_BANK_STARTS[u // G][u % G // 2] + BANK_PERIODS[u // G] * r: (u, r)
-            for u in range(1, UNITS, 2)
-            for r in range(PACK)
-        }
-        two_banks = [(u, r) for u in range(0, UNITS, 2) for r in range(PACK)]
-        for place in range(max(one_bank)):
-            if place not in one_bank and not two_banks:
+        steps_done = [0] * UNITS
+        columns_read = 0
+        read_end = {}
+        waiting = []
+
+        def bank_ready(u):
+            g = u % G
+            started_in_turn = u < G or steps_done[u - G] == PACK
+            since = columns_read - read_end.get((g, fills[g] % Z_BANKS[g]), -N)
+            return steps_done[u] < PACK and started_in_turn and since >= HALF - after_lead(u) + REFILL_MARGIN
+
+        while min(steps_done) < PACK:
+            ready = [u for u in PRECEDENCE if bank_ready(u)]
+            if not ready:
                 cast_w2(on_scalar, W2_SPLIT, G)
+                quantise_w2(W2_SPLIT, G)
+                columns_read = columns_read + (G - W2_SPLIT) * M * PACK
                 continue
-            u, r = one_bank[place] if place in one_bank else two_banks.pop(0)
-            first_layer(u, [r], after_lead(u), HALF)
-            if r == PACK - 1 and u < last - 1:
+            u = ready[0]
+            bank_key = (u % G, fills[u % G] % Z_BANKS[u % G])
+            first_layer(u, [steps_done[u]], after_lead(u), HALF)
+            steps_done[u] = steps_done[u] + 1
+            columns_read = columns_read + HALF - after_lead(u)
+            read_end[bank_key] = columns_read
+            if steps_done[u] == PACK and u < last:
                 scale_h(u, after_lead(u), HALF)
                 if u == 0:
                     quantise_w2(0, W2_SPLIT)
                     quantise_unit(0)
-                elif u > 1:
-                    quantise_unit(u - 1)
+                else:
+                    if waiting:
+                        quantise_unit(waiting.pop())
+                    waiting.append(u)
+        quantise_unit(waiting.pop())
 
-        scale_row(0)
-        first_layer(last, [PACK - 1], 0, HALF)
-        quantise_unit(last - 2)
-        scale_h(last - 1, 0, HALF)
-        quantise_w2(W2_SPLIT, G)
-        quantise_unit(last - 1)
-        second_layer(0, 0, HALF, on_scalar)
-        second_layer(1, 0, HALF, on_scalar)
-        scale_row(1)
-        scale_row(2)
-        second_layer(G, 0, HALF, on_scalar)
-        scale_row(3)
+        for r in range(PACK):
+            if r < Y_BANKS:
+                second_layer(r, 0, HALF, on_scalar)
+            scale_row(r)
         interleave_rows()
         for i in range(1, len(LAST_PIECES)):
             scale_h(last, *LAST_PIECES[i])
             quantise_h(*(word_of(last, c) for c in LAST_PIECES[i - 1]))
         quantise_h(*(word_of(last, c) for c in LAST_PIECES[-1]))
-        for u in (G + 1, 2, 3, G + 2):
+        for u in range(Y_BANKS, last):
             second_layer(u, 0, HALF, on_scalar)
         for c0, c1 in LAST_PIECES[:-1]:
             second_layer(last, c0, c1, on_scalar)

from contextlib import ExitStack

import concourse.mybir as mybir

G, D, K, M, N = 4, 128, 512, 128, 1024
FLOPS = 2 * G * D * K * N + 2 * G * K * M * N

F32 = mybir.dt.float32
BF16 = mybir.dt.bfloat16
U32 = mybir.dt.uint32
U8 = mybir.dt.uint8
FP8X4 = mybir.dt.float8_e4m3fn_x4

P = 128
PACK = 4
ROWS = D // PACK
QUAD = 32
NM = 128
HALF = 512
UNITS = G * N // HALF
RUN = 2
CAST_RUN = 4

LEAD = NM
X_LOADS = [(0, LEAD), (LEAD, 3 * LEAD), (3 * LEAD, HALF), (HALF, N)]
Z_BANKS = [2, 1, 1, 1]
Y_BANKS = 3
REFILL_MARGIN = 512
PRECEDENCE = [1, 0, 2, 3, 5, 4, 6, 7]
W2_SPLIT = 2
LAST_PIECES = [(0, 256), (256, 384), (384, 512)]


def tile_rows_gmlp_silu_bias_kernel(tc, x, w1, hs, w2, b, out):
    nc = tc.nc
    with ExitStack() as ctx:
        keep = ctx.enter_context(tc.tile_pool(name="keep", bufs=1))
        psum = ctx.enter_context(tc.psum_pool(name="psum", bufs=1))
        ctx.enter_context(tc.manual_schedule())

        def sb(name, shape, dtype):
            return keep.tile(shape, dtype, name=name, align_bytes=64)

        x_raw = [sb("x_raw%d" % i, [P, PACK, n1 - n0], F32) for i, (n0, n1) in enumerate(X_LOADS)]
        x_bf = sb("x_bf", [P, N * PACK], BF16)
        x_codes = sb("x_codes", [P, N], U32)
        x_scales = sb("x_scales", [P, N], U8)
        w1_raw = sb("w1_raw", [P, PACK, K], F32)
        w1_bf = sb("w1_bf", [P, K * PACK], BF16)
        w1_codes = sb("w1_codes", [P, K], U32)
        w1_scales = sb("w1_scales", [P, K], U8)
        w2_raw = sb("w2_raw", [P, G, PACK, M], F32)
        w2_bf = sb("w2_bf", [P, G * M * PACK], BF16)
        w2_codes = sb("w2_codes", [P, G * M], U32)
        w2_scales = sb("w2_scales", [P, G * M], U8)
        pitch = P // (G * G)
        vec_rows = sb("vec_rows", [P, P], F32)
        vec_dealt = sb("vec_dealt", [P, P], F32)
        vec_turned = sb("vec_turned", [P, P], F32)
        hs_sb = sb("hs_sb", [P, G, PACK], F32)
        act = [sb("act%d" % u, [P, PACK, HALF], F32) for u in range(UNITS)]
        h_bf = sb("h_bf", [P, G * N * PACK], BF16)
        h_codes = sb("h_codes", [P, G * N], U32)
        h_scales = sb("h_scales", [P, G * N], U8)
        h_rows = sb("h_rows", [P, PACK, LAST_PIECES[0][1]], BF16)
        result = [sb("result%d" % u, [P, HALF], F32) for u in range(UNITS)]
        z_banks = [[psum.tile([P, HALF], F32, name="bank_z%d_%d" % (g, i)) for i in range(Z_BANKS[g])] for g in range(G)]
        y_banks = [psum.tile([P, HALF], F32, name="bank_y%d" % i) for i in range(Y_BANKS)]

        idle = sb("idle", [P, 2], F32)
        nc.vector.memset(idle[:, 0:1], 0.0)
        nc.scalar.activation(out=idle[:, 1:2], in_=idle[:, 0:1], func=mybir.ActivationFunctionType.Silu)

        x_rows = x.rearrange("g (p j) n -> (g p) j n", j=PACK)
        w2_rows = w2.rearrange("g (p j) m -> p g (j m)", j=PACK)

        def load_x(i):
            nc.sync.dma_start(out=x_raw[i][:], in_=x_rows[:, :, X_LOADS[i][0] : X_LOADS[i][1]])

        nc.vector.memset(vec_rows[:], 0.0)
        nc.sync.dma_start(out=w1_raw[:], in_=w1.rearrange("g (p j) k -> (g p) j k", j=PACK))
        load_x(0)
        for e, vec in enumerate((b, hs)):
            nc.sync.dma_start(out=vec_rows[e:P:pitch, :], in_=vec.rearrange("g (q i) o -> q g (i o)", i=P))
        for i in range(1, len(X_LOADS)):
            load_x(i)
        for g0, g1 in ((0, W2_SPLIT), (W2_SPLIT, G)):
            nc.sync.dma_start(out=w2_raw[:, g0:g1].rearrange("p g j m -> p g (j m)"), in_=w2_rows[:, g0:g1])

        on_vector, on_scalar = nc.vector.tensor_copy, nc.scalar.copy

        def quantise(codes, scales, values, c0, c1):
            nc.vector.quantize_mx(out=codes[:, c0:c1].bitcast(FP8X4), scales=scales[:, c0:c1], in_=values[:, PACK * c0 : PACK * c1])

        def cast_w1(copy, r0, r1, s0, s1):
            dealt = w1_bf[:].rearrange("p (r s j) -> p s j r", r=PACK, j=PACK)
            raw = w1_raw[:].rearrange("p j (s r) -> p s j r", r=PACK)
            copy(out=dealt[:, s0:s1, :, r0:r1], in_=raw[:, s0:s1, :, r0:r1])

        def quantise_w1(r0, r1):
            quantise(w1_codes, w1_scales, w1_bf, r0 * P, r1 * P)

        def cast_x(i, copy=on_vector):
            n0, n1 = X_LOADS[i]
            copy(
                out=x_bf[:, PACK * n0 : PACK * n1].rearrange("p (c i j) -> p c j i", i=CAST_RUN, j=PACK),
                in_=x_raw[i][:].rearrange("p j (c i) -> p c j i", i=CAST_RUN),
            )

        def quantise_x(i):
            quantise(x_codes, x_scales, x_bf, *X_LOADS[i])

        def cast_w2(copy, g0, g1):
            copy(
                out=w2_bf[:, g0 * M * PACK : g1 * M * PACK].rearrange("p (g c i j) -> p g c j i", g=g1 - g0, i=CAST_RUN, j=PACK),
                in_=w2_raw[:, g0:g1].rearrange("p g j (c i) -> p g c j i", i=CAST_RUN),
            )

        def quantise_w2(g0, g1):
            quantise(w2_codes, w2_scales, w2_bf, g0 * M, g1 * M)

        fills = [0] * G

        def fill_bank(u, rs, c0, c1):
            g, n0, width = u % G, HALF * (u // G) + c0, c1 - c0
            bank = z_banks[g][fills[g] % Z_BANKS[g]]
            fills[g] += 1
            rows = slice(ROWS * g, ROWS * (g + 1))
            for slot, r in enumerate(rs):
                for c in range(0, width, NM):
                    nc.tensor.matmul_mx(
                        out=bank[:, slot * width + c : slot * width + c + NM],
                        lhsT=w1_codes[rows, r * P : (r + 1) * P].bitcast(FP8X4),
                        lhsT_scale=w1_scales[rows, r * P : (r + 1) * P],
                        rhs=x_codes[rows, n0 + c : n0 + c + NM].bitcast(FP8X4),
                        rhs_scale=x_scales[rows, n0 + c : n0 + c + NM],
                        start=True,
                        stop=True,
                    )
            return bank

        def empty_bank(bank, u, rs, c0, c1):
            width = c1 - c0
            for slot, r in enumerate(rs):
                b_column = QUAD * r + pitch * (u % G)
                nc.scalar.activation(
                    out=act[u][:, r, c0:c1],
                    in_=bank[:, slot * width : (slot + 1) * width],
                    func=mybir.ActivationFunctionType.Silu,
                    bias=vec_turned[:, b_column : b_column + 1],
                )

        def first_layer(u, rs, c0, c1):
            empty_bank(fill_bank(u, rs, c0, c1), u, rs, c0, c1)

        def after_lead(u):
            return LEAD if u < G else 0

        def word_of(u, c):
            if u >= G:
                return u * HALF + c
            return u * LEAD + c if c < LEAD else G * LEAD + u * (HALF - LEAD) + c - LEAD

        def scale_h(u, c0, c1):
            w0 = word_of(u, c0)
            nc.vector.tensor_tensor(
                out=h_bf[:, PACK * w0 : PACK * (w0 + c1 - c0)].rearrange("p (c i r) -> p c r i", i=RUN, r=PACK),
                in0=act[u][:, :, c0:c1].rearrange("p r (c i) -> p c r i", i=RUN),
                in1=hs_sb[:, u % G].unsqueeze(1).unsqueeze(3).to_broadcast([P, (c1 - c0) // RUN, PACK, RUN]),
                op=mybir.AluOpType.mult,
            )

        def scale_row(r):
            hs_column = QUAD * r + pitch * ((UNITS - 1) % G) + 1
            nc.scalar.activation(
                out=h_rows[:, r, :],
                in_=act[UNITS - 1][:, r, 0 : LAST_PIECES[0][1]],
                func=mybir.ActivationFunctionType.Copy,
                scale=vec_turned[:, hs_column : hs_column + 1],
            )

        def interleave_rows():
            w0 = word_of(UNITS - 1, 0)
            on_vector(
                out=h_bf[:, PACK * w0 : PACK * (w0 + LAST_PIECES[0][1])].rearrange("p (c i r) -> p c r i", i=CAST_RUN, r=PACK),
                in_=h_rows[:].rearrange("p r (c i) -> p c r i", i=CAST_RUN),
            )

        def quantise_h(w0, w1_end):
            quantise(h_codes, h_scales, h_bf, w0, w1_end)

        def quantise_unit(u):
            quantise_h(word_of(u, after_lead(u)), word_of(u, HALF - 1) + 1)

        results_made = []

        def second_layer(u, c0, c1, copy):
            g, n0 = u % G, HALF * (u // G)
            bank = y_banks[len(results_made) % Y_BANKS]
            results_made.append(u)
            for c in range(c0, c1, NM):
                w0 = word_of(u, c)
                nc.tensor.matmul_mx(
                    out=bank[:, c : c + NM],
                    lhsT=w2_codes[:, g * M : (g + 1) * M].bitcast(FP8X4),
                    lhsT_scale=w2_scales[:, g * M : (g + 1) * M],
                    rhs=h_codes[:, w0 : w0 + NM].bitcast(FP8X4),
                    rhs_scale=h_scales[:, w0 : w0 + NM],
                    start=True,
                    stop=True,
                )
            copy(out=result[u][:, c0:c1], in_=bank[:, c0:c1])
            nc.sync.dma_start(out=out[g, :, n0 + c0 : n0 + c1], in_=result[u][:, c0:c1])

        cast_w1(on_vector, 0, 2, 0, P)
        cast_w1(on_scalar, 2, PACK, 0, P // 2)
        cast_w1(on_vector, 2, PACK, P // 2, P)
        cast_x(0, on_scalar)
        on_scalar(out=vec_dealt[:].rearrange("p (r c) -> p c r", r=PACK), in_=vec_rows[:].rearrange("p (c r) -> p c r", r=PACK))
        quantise_w1(0, 2)
        quantise_w1(2, PACK)
        quantise_x(0)
        nc.vector.transpose(out=vec_turned[:], in_=vec_dealt[:])
        cast_x(1)
        on_vector(out=hs_sb[:], in_=vec_turned[:].rearrange("p (r g e) -> p g r e", r=PACK, g=G)[:, :, :, 1])
        quantise_x(1)
        cast_x(2)

        first_layer(0, [0, 1], 0, LEAD)
        first_layer(0, [2, 3], 0, LEAD)
        scale_h(0, 0, LEAD)
        quantise_x(2)
        for g in range(1, G):
            first_layer(g, range(PACK), 0, LEAD)
            if g == G - 1:
                quantise_h(0, 2 * LEAD)
            scale_h(g, 0, LEAD)
        cast_x(3)
        quantise_h(2 * LEAD, G * LEAD)
        quantise_x(3)
        cast_w2(on_vector, 0, W2_SPLIT)

        last = UNITS - 1
        steps_done = [0] * UNITS
        columns_read = 0
        read_end = {}
        waiting = []

        def bank_ready(u):
            g = u % G
            started_in_turn = u < G or steps_done[u - G] == PACK
            since = columns_read - read_end.get((g, fills[g] % Z_BANKS[g]), -N)
            return steps_done[u] < PACK and started_in_turn and since >= HALF - after_lead(u) + REFILL_MARGIN

        while min(steps_done) < PACK:
            ready = [u for u in PRECEDENCE if bank_ready(u)]
            if not ready:
                cast_w2(on_scalar, W2_SPLIT, G)
                quantise_w2(W2_SPLIT, G)
                columns_read = columns_read + (G - W2_SPLIT) * M * PACK
                continue
            u = ready[0]
            bank_key = (u % G, fills[u % G] % Z_BANKS[u % G])
            first_layer(u, [steps_done[u]], after_lead(u), HALF)
            steps_done[u] = steps_done[u] + 1
            columns_read = columns_read + HALF - after_lead(u)
            read_end[bank_key] = columns_read
            if steps_done[u] == PACK and u < last:
                scale_h(u, after_lead(u), HALF)
                if u == 0:
                    quantise_w2(0, W2_SPLIT)
                    quantise_unit(0)
                else:
                    if waiting:
                        quantise_unit(waiting.pop())
                    waiting.append(u)
        quantise_unit(waiting.pop())

        for r in range(PACK):
            if r < Y_BANKS:
                second_layer(r, 0, HALF, on_scalar)
            scale_row(r)
        interleave_rows()
        for i in range(1, len(LAST_PIECES)):
            scale_h(last, *LAST_PIECES[i])
            quantise_h(*(word_of(last, c) for c in LAST_PIECES[i - 1]))
        quantise_h(*(word_of(last, c) for c in LAST_PIECES[-1]))
        for u in range(Y_BANKS, last):
            second_layer(u, 0, HALF, on_scalar)
        for c0, c1 in LAST_PIECES[:-1]:
            second_layer(last, c0, c1, on_scalar)
        second_layer(last, *LAST_PIECES[-1], on_vector)
